import numpy as np, ml_dtypes
CORES = [3,11,19,27,35,43,51,59]
N = 8
BF = ml_dtypes.bfloat16
W, L, OR, ST, NEED = 4096, 128, 16, 2, 10
def forest(rng):
    o = np.argsort(rng.random((N, 8, 16, L, OR)), axis=2); k = np.arange(16).reshape(1, 1, 16, 1, 1)
    q = (rng.random(o.shape) * k).astype(np.int64); p = np.zeros_like(o)
    np.put_along_axis(p, o, np.take_along_axis(o, q, 2), 2)
    return np.where(rng.random(p.shape) < 0.1, k, p)
def limits(rng, lo, n):
    base = np.argsort(rng.random((N, 8, 1, L)), axis=-1) % n + lo
    return np.clip(base + rng.integers(-2, 3, (N, 8, 16, L)), 0, 15)
def parts(rng):
    x = rng.integers(0, 16, (N, 8, 16, W)); c = rng.integers(0, W, (N, 8, 16, L, OR)); p = forest(rng); a = limits(rng, 3, 8)
    v = rng.integers(0, 33, (N, 8, OR, L))
    o = np.arange(OR).reshape(1, 1, OR, 1); fav = rng.integers(0, OR, (1, 8, 1, L)); stick = rng.random((1, 8, 1, L)) < 0.5
    v = np.where(stick, np.where(o == fav, rng.integers(20, 33, v.shape), rng.integers(0, 7, v.shape)), v)
    return x, c, p, a, v
def bf(a): return np.ascontiguousarray(a).astype(np.float32).astype(BF)
def pack(x, c, p, a, v):
    return {"xt": bf(x.reshape(N, 128, W)), "pg": np.ascontiguousarray(c.reshape(N, 128, L * OR)).astype(np.int32), "pre": bf(p.reshape(N, 128, L * OR)),
            "lim": bf(a.reshape(N, 128, L)), "vv": np.ascontiguousarray(v.reshape(N, 8 * OR, L)).astype(np.int32)}
def setup_inputs(rng):
    return pack(*parts(rng))
def setup_inputs_ties(rng):
    x, c, p, a, v = parts(rng)
    dl = rng.integers(1, 8, (1, 8, 1, 1)); x = rng.integers(0, 9, (N, 8, 16, 1)) + dl * rng.integers(0, 2, x.shape)
    k = np.argsort(rng.random((N, 8, 1, L)), axis=-1) % 5; n = np.array([0, 2 * NEED - 16, 2 * NEED - 15, NEED - 1, 16])[k]
    a = np.where(np.argsort(rng.random(a.shape), axis=2) < n, dl, dl - 1)
    t = rng.choice(np.array([0, 1, 16, 31, 32]), (N, 8, 1, L))
    v = np.where(np.argsort(rng.random(v.shape), axis=2) < 2, t, np.minimum(rng.integers(0, 33, v.shape), t))
    return pack(x, c, p, a, v)
def setup_inputs_ends(rng):
    x, c, p, a, v = parts(rng)
    x = 15 * rng.integers(0, 2, x.shape); x[..., 0] = 0; x[..., W - 1] = 15
    e = rng.choice(np.array([0, 1, W // 2, W - 2, W - 1]), c.shape); c = np.where(rng.random((N, 8, 1, L, 1)) < 0.5, e, c)
    T = np.arange(16).reshape(1, 1, 16, 1, 1); k = rng.integers(0, 6, (N, 8, 1, L, 1))
    q = np.where(k == 0, T, np.where(k == 1, np.maximum(T - 1, 0), np.where(k == 2, 0, np.where(k == 3, 15, (T + 1) % 16))))
    p = np.where(k == 5, rng.integers(0, 16, p.shape), q)
    k = np.argsort(rng.random((N, 8, 1, L)), axis=-1) % 5; pos = np.argsort(rng.random(a.shape), axis=2)
    a = np.where(k == 0, 0, np.where(k == 1, 15, np.where(k == 2, 14, np.where(pos < np.where(k == 3, NEED, NEED - 1), 15, 0))))
    o = np.arange(OR).reshape(1, 1, OR, 1); k = rng.integers(0, 5, (N, 8, 1, L))
    v = np.where(k == 0, 0, np.where(k == 1, 32, np.where(k == 2, 32 * (o == 0), np.where(k == 3, 32 * (o == OR - 1), v))))
    z = int(rng.integers(0, 8)); w = np.argsort(rng.random(L)) % 4; x[:, z] = 15 * (np.arange(W) & 1)
    tt = T[0]; ring = (w == 0).reshape(1, 1, L, 1); climb = (w == 1).reshape(1, 1, L, 1)
    par = rng.integers(0, 2, (N, 1, L, OR)); even = c[:, z] - (c[:, z] & 1)
    c[:, z] = np.where(ring, even + ((par + tt) & 1), np.where(climb, even + ((par + (tt == 15)) & 1), c[:, z]))
    p[:, z] = np.where(ring, (tt + 1) % 16, np.where(climb, 0, p[:, z]))
    a = np.where(w == 1, 15, a); a[:, z] = np.where(w <= 1, 14 * rng.integers(0, 2, (N, 16, L)), a[:, z])
    v[:, z] = np.where(w == 1, 32 * (o[0] < 5) - 1 * (o[0] == 3), v[:, z])
    return pack(x, c, p, a, v)
def setup_inputs_alike(rng):
    x, c, p, a, v = parts(rng)
    x[:, ::2] = x[:, ::2][..., rng.integers(0, 8, W)]
    few = rng.integers(0, W, 5); few[0] = 0; few[1] = W - 1; c = few[rng.integers(0, 5, c.shape)]
    m = (rng.random((N, 8, 1, L, 1)) < 0.3) | (rng.random((N, 1, 1, L, 1)) < 0.3)
    c = np.where(m, c[:, :, :1], c); a[:, rng.integers(0, 8)] = 0
    return pack(x, c, p, a, v)
def setup_inputs_same(rng):
    x, c, p, a, v = parts(rng)
    o = np.arange(OR).reshape(1, 1, OR, 1); fav = rng.integers(0, OR, (1, 8, 1, L))
    v = np.where(o == fav, 32, rng.integers(0, 3, v.shape)); a = limits(rng, 5, 6)
    a[:, rng.integers(0, 8)] = rng.integers(0, 5, (N, 16, L))
    return pack(x, c, p, a, v)
def setup_inputs_spread(rng):
    x, c, p, a, v = parts(rng); E = np.array([0.25, 0.5, 1.0, 2.0, 4.0])
    def un(n, shape, by): return np.minimum((n * rng.random(shape) ** rng.choice(E, by)).astype(np.int64), n - 1)
    x = un(16, x.shape, (N, 8, 16, 1)); c = un(W, c.shape, (N, 8, 1, L, OR)); a = un(16, a.shape, (N, 8, 1, L)); v = un(33, v.shape, (N, 8, OR, 1))
    return pack(x, c, p, a, v)
def check_inputs(d):
    bad = []
    for k, hi in (("xt", 15), ("pg", W - 1), ("pre", 15), ("lim", 15), ("vv", 32)):
        b = np.asarray(d[k]).astype(np.float64)
        if not (np.min(b) >= 0 and np.max(b) <= hi and np.all(b == np.floor(b))): bad.append("range of " + k)
    return bad
def reference(xt, pg, pre, lim, vv):
    xs = np.ascontiguousarray(xt.astype(np.int32).reshape(N, 8, 16, W).transpose(0, 1, 3, 2))
    cur = np.ascontiguousarray(pg.astype(np.int64).reshape(N, 8, 16, L, OR).transpose(0, 1, 3, 4, 2))
    prd = np.ascontiguousarray(pre.astype(np.int64).reshape(N, 8, 16, L, OR).transpose(0, 1, 3, 4, 2))
    a = np.ascontiguousarray(lim.astype(np.int32).reshape(N, 8, 16, L).transpose(0, 1, 3, 2))
    v = np.ascontiguousarray(vv.astype(np.int64).reshape(N, 8, OR, L).transpose(0, 1, 3, 2))
    m = np.zeros((N, 8, L), np.int64)
    g0 = np.arange(8).reshape(1, 8, 1); l0 = np.arange(L).reshape(1, 1, L)
    for s in range(N):
        h = ((np.arange(N) + s) % N).reshape(N, 1, 1)
        o = np.argmax(v, axis=3)
        c = cur[h, g0, l0, o]; p = prd[h, g0, l0, o]
        got = np.zeros((N, 8, L), np.int64)
        for t in range(ST):
            F = xs[h[..., None], g0[..., None], c]
            G = np.take_along_axis(F, p[..., None], 3)
            D = np.abs(F - G)
            ok = np.add.reduce((D <= a[:, :, :, None, :]).astype(np.int64), axis=4) >= NEED
            full = np.all(ok, axis=3)
            got = got + full
            c = np.where(full[..., None], (5 * c + 1) & (W - 1), np.where(ok, c, (5 * c + np.add.reduce(D, axis=4) + 1) & (W - 1)))
        cur[h, g0, l0, o] = c
        m = m + got
        odd = np.add.reduce(got, axis=1, keepdims=True) & 1
        v = v + 1 + odd[..., None]
        np.put_along_axis(v, o[..., None], np.add.reduce(ok.astype(np.int64), axis=3)[..., None], 3)
    return {"yg": np.ascontiguousarray(cur.transpose(0, 1, 4, 2, 3)).reshape(N, 128, L * OR).astype(np.float32),
            "yv": np.ascontiguousarray(v.transpose(0, 1, 3, 2)).reshape(N, 8 * OR, L).astype(np.float32), "ym": m.astype(np.float32)}

@@ -1,0 +1,440 @@
+from concourse.bass import DstId, RemoteDMATransfer
+from concourse.mybir import AluOpType as ALU, AxisListType, ActivationFunctionType as AF
+
+N, NB = 8, 2
+LB = 128 // NB
+H = LB // 16
+LS = 16
+NS = LB // LS
+CB, CS = 16 * LB, 16 * LS
+MW = LB + 16
+GS = ((1, NS - 1),)
+BON, LOOK, HOLD = 3.0, 0.1, 0.4
+KB = 1 << 19
+W15 = 1 << 15
+THR = 10 * W15
+
+SCRATCH = {
+    "xw": ("sbuf", [128, 4096], "bfloat16"), "pw": ("sbuf", [128, 2048], "bfloat16"),
+    "pgi": ("sbuf", [128, 2048], "int32"), "cw": ("sbuf", [128, 2048], "float32"),
+    "vt": ("sbuf", [128, 128], "int32"), "vtb": ("sbuf", [128, 128], "bfloat16"),
+    "limo": ("sbuf", [128, 128], "bfloat16"), "limt": ("sbuf", [128, 128 * N], "bfloat16"),
+    "minb": ("sbuf", [128, MW * NB * (N + 1)], "float32"), "mout": ("sbuf", [128, MW * NB * N], "float32"),
+    "mia": ("sbuf", [128, 8 * NB * N], "int32"), "mxo": ("sbuf", [128, 8 * NB * N], "int32"),
+    "onef": ("sbuf", [128, 128], "float32"), "oneb": ("sbuf", [128, 128], "bfloat16"), "posb": ("sbuf", [128, 128], "bfloat16"),
+    "bias": ("sbuf", [128, 1], "float32"),
+    "idf": ("sbuf", [128, 128], "float32"), "idb": ("sbuf", [128, 128], "bfloat16"), "nid": ("sbuf", [128, 128], "bfloat16"),
+    "idp": ("sbuf", [128, 128], "float32"), "idn": ("sbuf", [128, 128], "float32"),
+    "bo0": ("sbuf", [128, 128], "bfloat16"), "bo": ("sbuf", [128, 128], "bfloat16"),
+    "bq1": ("sbuf", [128, 128], "float32"), "bq2": ("sbuf", [128, 128], "float32"), "bq": ("sbuf", [128, 128], "bfloat16"),
+    "pmt": ("sbuf", [128, 128], "bfloat16"), "es": ("sbuf", [128, 2048], "bfloat16"), "ew": ("sbuf", [128, 2048], "bfloat16"),
+    "ex": ("sbuf", [128, 2048], "bfloat16"),
+    "ix": ("sbuf", [128, 128], "int32"), "ix2": ("sbuf", [128, 128], "int32"), "ml": ("sbuf", [128, 128], "bfloat16"),
+    "ka": ("sbuf", [128, LB], "int32"), "ka2": ("sbuf", [128, LB], "int32"), "kb": ("sbuf", [128, LB], "int32"), "ck": ("sbuf", [128, LB], "float32"),
+    "r16": ("sbuf", [128, LB], "bfloat16"), "cli": ("sbuf", [128, H], "int32"), "cli2": ("sbuf", [128, H], "int32"), "cl": ("sbuf", [128, H], "uint16"),
+    "e4a": ("sbuf", [128, LB], "bfloat16"), "e4": ("sbuf", [128, LB], "bfloat16"), "e4s": ("sbuf", [128, LB], "bfloat16"), "e4n": ("sbuf", [128, LB], "bfloat16"),
+}
+TILE = {"f": (CB, "bfloat16"), "gq": (CB, "bfloat16"), "a": (CB, "bfloat16"), "m": (CB, "bfloat16"), "li": (4, "int32"), "ls": (4, "uint16"),
+        "cf": (LB, "float32"), "co": (LB, "uint16"), "lk": (4, "float32"), "mo": (4, "float32"), "pg_": (LB, "bfloat16"), "po": (LB, "uint16"),
+        "a5": (LB, "float32"), "ax": (LB, "float32"), "pa": (LB, "bfloat16"), "bm": (LB, "float32"), "yi": (LB, "int32"), "ci": (LB, "int32"),
+        "f8": (16, "bfloat16"), "mm": (4, "float32"), "mn": (4, "int32"), "od": (4, "int32"), "rb": (LB, "bfloat16"), "mk": (128, "bfloat16"),
+        "ns": (LB, "float32"), "se": (LB, "float32"), "ua": (LB, "float32"), "vo": (128, "float32"), "yo": (LB, "float32")}
+for _n in TILE:
+    SCRATCH[_n] = ("sbuf", [128, NB * TILE[_n][0]], TILE[_n][1])
+for _b in range(8):
+    SCRATCH["pb%d" % _b] = ("psum", [128, 512], "float32")
+
+SEMAPHORES = ["qv", "qs", "qt", "qg", "lsem", "limr", "dlim", "dvv", "dxt"]
+SEMAPHORES += ["%s%d" % (n, b) for n in ("dpg", "dpre", "oyg", "oyv", "oym") for b in range(NB)]
+SEMAPHORES += ["h%d_%d" % (s, b) for s in range(1, N + 1) for b in range(NB)] + ["k%d_%d" % (s, b) for s in range(1, N) for b in range(NB)]
+
+CYC, FAC, WAKE, XG, PEC, HOP = 0.00083, 1.0, 0.2, 1.56, 0.0004, 4.0
+
+
+def cv(n):
+    return max(64, n) * CYC * FAC
+
+
+def cg(n):
+    return (0.055 + XG * n * CYC) * FAC
+
+
+def ct(n):
+    return n * PEC
+
+
+def schedule(nodes):
+    n = len(nodes)
+    succ = [[] for _ in range(n)]
+    for i, d in enumerate(nodes):
+        for j in d["dep"]:
+            succ[j].append(i)
+    pri = [0.0] * n
+    for i in range(n - 1, -1, -1):
+        d = nodes[i]
+        pri[i] = d["c"] + d["lat"] + WAKE + max([pri[k] for k in succ[i]] + [0.0])
+    for i in range(n):
+        pri[i] -= nodes[i]["bl"]
+    left = [len(d["dep"]) for d in nodes]
+    ready = [0.0] * n
+    free = {"v": 0.0, "s": 0.0, "t": 0.0, "g": 0.0, "y": 0.0}
+    pool = {q: [] for q in list(free) + ["r"]}
+    for i in range(n):
+        if left[i] == 0:
+            pool[nodes[i]["q"]].append(i)
+    order = []
+    while len(order) < n:
+        best = None
+        for q in pool:
+            if not pool[q]:
+                continue
+            f = free.get(q, 0.0)
+            t0 = min(max(f, ready[i]) for i in pool[q])
+            i = max((i for i in pool[q] if max(f, ready[i]) <= t0 + LOOK), key=lambda i: pri[i])
+            e0 = max(f, ready[i]) + HOLD * nodes[i]["c"]
+            i = max((j for j in pool[q] if ready[j] <= e0), key=lambda j: pri[j])
+            st = max(f, ready[i])
+            if best is None or st < best[0]:
+                best = (st, q, i)
+        st, q, i = best
+        pool[q].remove(i)
+        en = st + nodes[i]["c"]
+        if q != "r":
+            free[q] = en
+        order.append(i)
+        for k in succ[i]:
+            w = 0.0 if (nodes[k]["q"] == q and not nodes[k]["dep"][i]) else WAKE
+            ready[k] = max(ready[k], en + nodes[i]["lat"] + w)
+            left[k] -= 1
+            if left[k] == 0:
+                pool[nodes[k]["q"]].append(k)
+    return order
+
+
+def rank_program(g, core, T, topo):
+    rank = T.rank_of(core)
+    if rank is None:
+        return
+    eng = {"v": g.vector, "s": g.scalar, "t": g.tensor, "g": g, "y": g.sync}
+    csem = {"v": "qv", "s": "qs", "t": "qt", "g": "qg"}
+    nodes, last, cur = [], {}, [0.0]
+    STREAM = ("ls", "co", "po", "cw", "f")
+
+    def add(q, fns, R=(), W=(), c=0.08, sem=None, val=None, after=(), lat=0.0):
+        i = len(nodes)
+        dep = {}
+        for (acc, wr) in ((R, False), (W, True)):
+            for (buf, a, b) in acc:
+                bank = buf[:2] == "pb"
+                rec = last.setdefault(buf, [])
+                for (j, ja, jb, jw) in rec:
+                    if j == i or (not bank and (ja >= b or jb <= a)):
+                        continue
+                    same = nodes[j]["q"] == q
+                    if not (wr or jw) and (same or not bank):
+                        continue
+                    need = not (same and (q == "t" or not (jw or buf in STREAM)))
+                    dep[j] = dep.get(j, False) or need
+                if wr:
+                    if bank and q == "t":
+                        rec[:] = [r for r in rec if r[0] == i]
+                    elif not bank:
+                        rec[:] = [r for r in rec if r[0] == i or not (r[1] >= a and r[2] <= b)]
+                rec.append((i, a, b, wr))
+        for j in after:
+            dep[j] = dep.get(j, False)
+        nodes.append({"q": q, "f": fns if isinstance(fns, list) else [fns], "dep": dep, "c": c, "sem": sem, "val": val, "lat": lat, "bl": cur[0]})
+        return i
+
+    t = T
+    nm = lambda n, b: "%s%d" % (n, b)
+    v, sc, te = g.vector, g.scalar, g.tensor
+    IDF, CK, IDB, NID, BO, ML, E4 = ("idf", 0, 128), ("ck", 0, LB), ("idb", 0, 128), ("nid", 0, 128), ("bo", 0, 128), ("ml", 0, 128), ("e4", 0, LB)
+
+    def load(fns, W, sem, cost, q="y"):
+        add(q, fns, (), W, 0.06 * len(fns), sem, 16 * len(fns), (), cost)
+    load([lambda k=k: g.scalar.dma_start(t.vt[:, 16 * k:16 * k + 16], t.vv[16 * k:16 * k + 16, :]) for k in range(8)], [("vt", 0, 128)], "dvv", 3.0, "s")
+    load([lambda: g.sync.dma_start(t.limo[:], t.lim[:])], [("limo", 0, 128)], "dlim", 2.5)
+    for b in range(NB):
+        load([lambda b=b: g.sync.dma_start(t.pgi[:, CB * b:CB * b + CB], t.pg[:, CB * b:CB * b + CB])], [("pgi", CB * b, CB * b + CB)], nm("dpg", b), 4.5 + 5.5 * b)
+        if b == 0:
+            load([lambda: g.sync.dma_start(t.xw[:], t.xt[:])], [("xw", 0, 4096)], "dxt", 7.0)
+        load([lambda b=b: g.sync.dma_start(t.pw[:, CB * b:CB * b + CB], t.pre[:, CB * b:CB * b + CB])], [("pw", CB * b, CB * b + CB)], nm("dpre", b), 7.5 + 4.0 * b)
+
+    def vmem(buf, a, b, val):
+        add("v", lambda: v.memset(t[buf][:, a:b], val), (), [(buf, a, b)], cv((b - a) * (0.5 if SCRATCH[buf][2] == "bfloat16" else 1)))
+
+    def vts(out, in0, n, fn, half=False):
+        add("v", fn, [(in0, 0, n)], [(out, 0, n)], cv(n * (0.5 if half else 1)))
+
+    def gen(out, n, fn, in_=None):
+        add("g", fn, [(in_, 0, n)] if in_ else (), [(out, 0, n)], (0.17 + 2 * n * CYC) * FAC)
+    vmem("onef", 0, 128, 1.0)
+    vmem("oneb", 0, 128, 1.0)
+    vmem("posb", 0, 128, 1024.0)
+    vmem("bias", 0, 1, -15.0)
+    gen("idf", 128, lambda: g.affine_select(t.idf[:], t.onef[:], [[-1, 128]], ALU.is_equal, 0.0, 0, 1), "onef")
+    gen("pmt", 128, lambda: g.affine_select(t.pmt[:], t.posb[:], [[-H, NB], [-8, 16], [-1, H]], ALU.is_equal, 0.0, 0, 1), "posb")
+    gen("ka", LB, lambda: g.iota(t.ka[:], [[0, LB]], 0, 16))
+    gen("kb", LB, lambda: g.iota(t.kb[:], [[-1, 16], [-256, H]], 65536 + 1023, 0))
+    gen("cli", H, lambda: g.iota(t.cli[:], [[0, H]], 0, 1))
+    gen("r16", LB, lambda: g.iota(t.r16[:], [[0, NS], [16, LS]], 0, 0, allow_small_or_imprecise_dtypes=True))
+    gen("bo0", 128, lambda: g.affine_select(t.bo0[:], t.oneb[:], [[-16, 8], [0, 16]], ALU.is_ge, 0.0, 0, 1), "oneb")
+    gen("bo", 128, lambda: g.affine_select(t.bo[:], t.bo0[:], [[16, 8], [0, 16]], ALU.is_ge, 0.0, 15, -1), "bo0")
+    gen("es", 2048, lambda: g.iota(t.es[:], [[0, 2048]], 0, 0, allow_small_or_imprecise_dtypes=True))
+    gen("ix", 128, lambda: g.iota(t.ix[:], [[-1, 128]], 128, 1))
+    gen("e4a", LB, lambda: g.affine_select(t.e4a[:], t.oneb[:, 0:LB], [[0, 16], [-16, H]], ALU.is_ge, 0.0, 0, 1), "oneb")
+    gen("e4", LB, lambda: g.affine_select(t.e4[:], t.e4a[:], [[0, 16], [16, H]], ALU.is_ge, 0.0, 15, -1), "e4a")
+    gen("mout", MW * NB * N, lambda: g.iota(t.mout[:], [[0, MW * NB * N]], 0, 0, allow_small_or_imprecise_dtypes=True))
+    vts("idb", "idf", 128, lambda: v.tensor_copy(t.idb[:], t.idf[:]))
+    add("v", lambda: v.tensor_copy(t.vtb[:], t.vt[:]), [("vt", 0, 128)], [("vtb", 0, 128)], cv(128))
+    vts("ka2", "ka", LB, lambda: v.tensor_scalar(t.ka2[:], t.ka[:], 255, None, ALU.bitwise_and))
+    add("v", lambda: v.tensor_tensor(t.ck[:], t.kb[:], t.ka2[:], ALU.subtract), [("ka2", 0, LB), ("kb", 0, LB)], [CK], cv(2 * LB))
+    vts("cli2", "cli", H, lambda: v.tensor_scalar(t.cli2[:], t.cli[:], H - 1, None, ALU.bitwise_and))
+    vts("cl", "cli2", H, lambda: v.tensor_copy(t.cl[:], t.cli2[:]))
+    for b in range(NB):
+        add("v", lambda b=b: v.tensor_copy(t.cw[:, CB * b:CB * b + CB], t.pgi[:, CB * b:CB * b + CB]), [("pgi", CB * b, CB * b + CB)], [("cw", CB * b, CB * b + CB)], cv(CB))
+
+    def mi(s, b):
+        return MW * (NB * s + b)
+    for b in range(NB):
+        o = mi(0, b)
+        pb = nm("pb", 6 + b)
+        add("t", [lambda b=b, pb=pb: te.matmul(t[pb][:, 448:448 + LB], t.vtb[:], t.pmt[:, LB * b:LB * b + LB], True, True)],
+            [("vtb", 0, 128), ("pmt", 0, 128)], [(pb, 0, 512)], ct(64))
+        add("v", lambda o=o, pb=pb: v.tensor_tensor(t.minb[:, o:o + LB], t.ck[:], t[pb][:, 448:448 + LB], ALU.add), [(pb, 0, 512), CK], [("minb", o, o + LB)], cv(LB))
+        vmem("minb", o + LB, o + MW, 0.0)
+        for j in range(H):
+            add("v", lambda j=j, b=b, o=o: v.tensor_reduce(t.mia[:, 8 * b + j:8 * b + j + 1], t.minb[:, o + j:o + LB:H], AxisListType.X, ALU.max),
+                [("minb", o, o + LB)], [("mia", 8 * b + j, 8 * b + j + 1)], cv(16))
+    add("t", lambda: te.matmul(t.pb0[:, 0:128], t.limo[:], t.idb[:], True, True), [("limo", 0, 128), IDB], [("pb0", 0, 512)], ct(128))
+    add("s", lambda: sc.activation(t.limt[:, 0:128], t.pb0[:, 0:128], AF.Copy), [("pb0", 0, 512)], [("limt", 0, 128)], cv(128))
+    nxt = T.cores[(rank + 1) % N]
+    nrid, npid, _ = topo.addr(nxt)
+    nmask = topo.mask(core, nxt)
+    nne = bin(nmask).count("1")
+    dst, dsts, mask = [], [], nmask
+    for s in range(1, N):
+        d = T.cores[(rank + s) % N]
+        rid, pid, _ = topo.addr(d)
+        mask &= topo.mask(core, d)
+        dst.append(DstId(rid=rid, pnc=pid))
+        dsts.append(t.limt[:, 128 * s:128 * s + 128])
+    ne = bin(mask).count("1")
+    limsend = add("g", lambda: g.remote_dma_fused([RemoteDMATransfer(dst_ids=dst, dma_engine_mask=mask, remote_sem=t.sem.limr,
+                  srcs=[t.limt[:, 0:128]], dsts=dsts)], local_sem=t.sem.lsem), [("limt", 0, 128)], (), 2.0, "lsem", -ne)
+    add("r", [], (), [("limt", 128, 128 * N)], 4.0, "limr", 7 * ne, (limsend,))
+
+    for k in range(16):
+        add("s", lambda k=k: sc.activation(t.ex[:, k::16], t.idb[:], AF.Copy), [IDB], [("ex", 0, 2048)], cv(128))
+    for k in range(16):
+        add("v", lambda k=k: v.tensor_copy(t.es[:, 128 * k + k:128 * k + 128:16], t.bo[:, k::16]), [BO], [("es", 128 * k, 128 * k + 128)], cv(8))
+    add("v", lambda: v.tensor_scalar(t.ew[:], t.es[:], float(W15), None, ALU.mult), [("es", 0, 2048)], [("ew", 0, 2048)], cv(1024))
+    vts("bq1", "idb", 128, lambda: v.tensor_scalar(t.bq1[:], t.idb[:], float(-32 * KB), None, ALU.mult))
+    vts("bq2", "bo", 128, lambda: v.tensor_scalar(t.bq2[:], t.bo[:], float(KB), None, ALU.mult))
+    add("v", lambda: v.tensor_tensor(t.bq[:], t.bq1[:], t.bq2[:], ALU.add), [("bq1", 0, 128), ("bq2", 0, 128)], [("bq", 0, 128)], cv(256))
+    vts("nid", "idb", 128, lambda: v.tensor_scalar(t.nid[:], t.idb[:], -1.0, None, ALU.mult), True)
+    vts("ix2", "ix", 128, lambda: v.tensor_scalar(t.ix2[:], t.ix[:], 15, None, ALU.bitwise_and))
+    vts("ml", "ix2", 128, lambda: v.tensor_scalar(t.ml[:], t.ix2[:], 0.0, None, ALU.is_equal))
+    vts("e4s", "e4", LB, lambda: v.tensor_scalar(t.e4s[:], t.e4[:], -1024.0, None, ALU.mult), True)
+    vts("e4n", "e4", LB, lambda: v.tensor_scalar(t.e4n[:], t.e4[:], 1024.0, None, ALU.mult), True)
+    vts("idp", "idf", 128, lambda: v.tensor_scalar(t.idp[:], t.idf[:], 1.0 / 1024, None, ALU.mult))
+    vts("idn", "idf", 128, lambda: v.tensor_scalar(t.idn[:], t.idf[:], -1.0 / 1024, None, ALU.mult))
+
+    def tiles(b):
+        def L(n, a=0, e=None):
+            w = TILE[n][0]
+            return (n, w * b + a, w * b + (w if e is None else e))
+
+        def X(n, a=0, e=None, p=128, st=1):
+            _, c0, c1 = L(n, a, e)
+            return t[n][0:p, c0:c1:st] if st > 1 else t[n][0:p, c0:c1]
+        return L, X, [nm("pb", 2 * b), nm("pb", 2 * b + 1)], nm("pb", 4 + b), nm("pb", 6 + b)
+    ALL = lambda bank: (bank, 0, 512)
+
+    def slice_block(s, b):
+        L, X, LX, RB, QB = tiles(b)
+        o, q0 = mi(s, b), MW * (NB * s + b)
+        U, UR = t.minb[:, o:o + LB], ("minb", o, o + LB)
+        cs, ce = CB * b, CB * b + CB
+        k0 = 8 * (NB * s + b)
+        MI, MIR = t.mia[:, k0:k0 + H], ("mia", k0, k0 + H)
+        add("v", lambda: v.tensor_scalar(X("li", 0, H), MI, 1023, None, ALU.bitwise_and), [MIR], [L("li")], cv(H))
+        add("v", lambda: v.tensor_scalar(X("ls", 0, H), X("li", 0, H), -1.0, 1023.0, ALU.mult, ALU.add), [L("li")], [L("ls")], cv(H))
+        add("v", lambda: v.tensor_copy(X("co"), t.cw[:, cs:ce].indirect(X("ls", 0, H))), [("cw", cs, ce), L("ls")], [L("co")], cg(LB))
+        add("s", lambda: sc.activation(X("cf"), t.cw[:, cs:ce].indirect(X("ls", 0, H)), AF.Copy), [("cw", cs, ce), L("ls")], [L("cf")], cg(LB))
+        add("s", lambda: sc.activation(X("pg_"), t.pw[:, cs:ce].indirect(X("ls", 0, H)), AF.Copy), [("pw", cs, ce), L("ls")], [L("pg_")], cg(LB))
+        add("t", [lambda: te.matmul(t[QB][:, 64:64 + LB], t.idb[:], X("pg_"), True, False), lambda: te.matmul(t[QB][:, 64:64 + LB], t.idb[:], t.r16[:], False, True)],
+            [IDB, L("pg_"), ("r16", 0, LB)], [ALL(QB)], ct(128))
+        add("v", lambda: v.tensor_copy(X("po"), t[QB][:, 64:64 + LB]), [ALL(QB)], [L("po")], cv(LB))
+        for h in range(2):
+            add("t", lambda h=h: te.matmul(t[LX[h]][:], t.limt[:, 128 * s:128 * s + 128], t.ex[:, cs + 512 * h:cs + 512 * h + 512], True, True),
+                [("limt", 128 * s, 128 * s + 128), ("ex", 0, 2048)], [ALL(LX[h])], ct(512))
+
+        def piece(st, u):
+            p0, p1, l0, l1 = CS * u, CS * u + CS, LS * u, LS * u + LS
+            lb, c0, DB = LX[p0 // 512], p0 % 512, (QB, RB)[u % 2]
+            win = lambda: X("f", p0, p1).indirect(X("po", l0, l1))
+            add("s", lambda: sc.activation(X("f", p0, p1), t.xw[:].indirect(X("co", l0, l1)), AF.Copy), [("xw", 0, 4096), L("co", l0, l1)], [L("f", p0, p1)], cg(CS))
+            gio = [L("f", p0, p1), L("po", l0, l1)], [L("gq", p0, p1)], cg(CS)
+            if (st, u) in GS:
+                add("s", lambda: sc.activation(X("gq", p0, p1), win(), AF.Copy), *gio)
+            else:
+                add("v", lambda: v.tensor_copy(X("gq", p0, p1), win()), *gio)
+            add("t", [lambda: te.matmul(t[DB][:, 256:256 + CS], t.idb[:], X("f", p0, p1), True, False), lambda: te.matmul(t[DB][:, 256:256 + CS], t.nid[:], X("gq", p0, p1), False, True)],
+                [IDB, NID, L("f", p0, p1), L("gq", p0, p1)], [ALL(DB)], ct(2 * CS))
+            add("s", lambda: sc.activation(X("a", p0, p1), t[DB][:, 256:256 + CS], AF.Abs), [ALL(DB)], [L("a", p0, p1)], cv(CS))
+            add("v", lambda: v.tensor_tensor(X("m", p0, p1), X("a", p0, p1), t[lb][:, c0:c0 + CS], ALU.is_le), [L("a", p0, p1), ALL(lb)], [L("m", p0, p1)], cv(CS))
+
+        def key_and_hop():
+            add("t", lambda: te.matmul(t[QB][0:LB, 232:240], X("pa"), t.bo[:, 0::16], True, True), [L("pa"), BO], [ALL(QB)], ct(64))
+            add("t", lambda: te.matmul(t[LX[1]][0:LB, 0:128], X("pa"), t.bo[:], True, True), [L("pa"), BO], [ALL(LX[1])], ct(128))
+            add("s", lambda: sc.activation(X("f8", 0, 16, LB), t[QB][0:LB, 224:240], AF.Relu, bias=t.bias[0:LB, 0:1], accum_out=X("mm", 0, 1, LB)),
+                [ALL(QB), ("bias", 0, 1)], [L("f8"), L("mm")], cv(64) + 0.02)
+            add("v", lambda: v.tensor_tensor(X("mk", 0, 128, LB), t.ml[0:LB, :], t[LX[1]][0:LB, 0:128], ALU.mult), [ALL(LX[1]), ML], [L("mk")], cv(128))
+            add("v", lambda: v.tensor_copy(X("mn", 0, 1, LB), X("mm", 0, 1, LB)), [L("mm")], [L("mn")], cv(1))
+            add("v", lambda: v.tensor_scalar(X("od", 0, 1, LB), X("mn", 0, 1, LB), 1, None, ALU.bitwise_and), [L("mn")], [L("od")], cv(1))
+            add("v", lambda: v.tensor_scalar(t.mout[0:LB, q0 + LB:q0 + LB + 1], X("od", 0, 1, LB), t.minb[0:LB, o + LB:o + LB + 1], 1.0, ALU.add, ALU.add),
+                [L("od"), ("minb", o + LB, o + LB + 8)], [("mout", q0 + LB, q0 + LB + 4)], cv(1))
+            add("v", lambda: v.tensor_scalar(X("rb", 0, LB, LB), t.e4s[0:LB, :], t.mout[0:LB, q0 + LB:q0 + LB + 1], None, ALU.mult),
+                [("mout", q0 + LB, q0 + LB + 4), ("e4s", 0, LB)], [L("rb")], cv(LB))
+            add("v", lambda: v.tensor_tensor(X("ns"), MI.indirect(t.cl[:, 0:H]), U, ALU.not_equal), [MIR, ("cl", 0, H), UR], [L("ns")], cg(LB))
+            add("s", lambda: sc.activation(X("se"), X("ns"), AF.Copy, bias=1.0, scale=-1.0), [L("ns")], [L("se")], cv(LB))
+            add("v", lambda: v.tensor_tensor(X("ua"), X("ns"), U, ALU.mult), [L("ns"), UR], [L("ua")], cv(2 * LB))
+            N0, N1, S0, S1 = 384, 384 + H, slice(256, 256 + LB), slice(320, 320 + LB)
+            if s < N - 1:
+                for j in range(H):
+                    add("v", lambda j=j: v.tensor_reduce(X("mo", j, j + 1), X("ua", j, None, 128, H), AxisListType.X, ALU.max), [L("ua")], [L("mo", j, j + 1)], cv(16))
+                add("v", lambda: v.tensor_scalar(X("lk", 0, H), X("li", 0, H), 65536.0, None, ALU.add), [L("li")], [L("lk")], cv(4))
+                add("t", [lambda: te.matmul(t[LX[0]][:, N0:N1], t.idf[:], X("lk", 0, H), True, False),
+                          lambda: te.matmul(t[LX[0]][:, N0:N1], X("mk", 0, 128, LB), t.e4n[0:LB, 0:H], False, False)],
+                    [IDF, L("lk"), L("mk"), ("e4n", 0, LB)], [ALL(LX[0])], ct(320))
+                add("t", lambda: te.matmul(t[LX[0]][:, N0:N1], t.ml[0:LB, :], X("rb", 0, H, LB), False, True), [ML, L("rb")], [ALL(LX[0])], ct(64))
+                add("v", lambda: v.tensor_tensor(t.mxo[:, k0:k0 + H], X("mo", 0, H), t[LX[0]][:, N0:N1], ALU.max), [ALL(LX[0]), L("mo")], [("mxo", k0, k0 + H)], cv(8))
+                k1, ks = k0 + 8 * NB, "k%d_%d" % (s + 1, b)
+                snd = add("g", lambda: g.remote_dma(t.mia[:, k1:k1 + H], t.mxo[:, k0:k0 + H], t.sem[ks], t.sem.lsem, npid, nrid, nmask),
+                          [("mxo", k0, k0 + H)], (), 1.0, "lsem", -nne)
+                add("r", [], (), [("mia", k1, k1 + H)], HOP, ks, nne, (snd,))
+            add("t", [lambda: te.matmul(t[LX[0]][:, S0], t.idf[:], t.ck[:], True, False),
+                      lambda: te.matmul(t[LX[0]][:, S0], X("mk", 0, 128, LB), t.e4n[0:LB, :], False, False)],
+                [IDF, CK, L("mk"), ("e4n", 0, LB)], [ALL(LX[0])], ct(320))
+            add("t", lambda: te.matmul(t[LX[0]][:, S0], t.ml[0:LB, :], X("rb", 0, LB, LB), False, True), [ML, L("rb")], [ALL(LX[0])], ct(64))
+            add("v", lambda: v.tensor_tensor(t[LX[0]][:, S1], X("se"), t[LX[0]][:, S0], ALU.mult), [L("se"), ALL(LX[0])], [ALL(LX[0])], cv(LB))
+            add("v", lambda: v.tensor_tensor(t.mout[:, q0:q0 + LB], t[LX[0]][:, S1], X("ua"), ALU.add), [ALL(LX[0]), L("ua")], [("mout", q0, q0 + LB)], cv(LB))
+            add("t", [lambda: te.matmul(t[LX[1]][0:LB, 128:136], t.idf[0:LB, 0:LB], t.minb[0:LB, o + LB + 8:o + MW], True, False)] +
+                [lambda k=k: te.matmul(t[LX[1]][0:LB, 128:136], t.idb[0:LB, 0:LB], X("f8", 8 * k, 8 * k + 8, LB), False, k == 1) for k in range(2)],
+                [IDF, IDB, ("minb", o + LB + 8, o + MW), L("f8")], [ALL(LX[1])], ct(384))
+            add("s", lambda: sc.activation(t.mout[0:LB, q0 + LB + 8:q0 + MW], t[LX[1]][0:LB, 128:136], AF.Copy), [ALL(LX[1])], [("mout", q0 + LB + 8, q0 + MW)], cv(64))
+            hs, no = "h%d_%d" % (s + 1, b), mi(s + 1, b)
+            snd = add("g", lambda: g.remote_dma(t.minb[:, no:no + MW], t.mout[:, q0:q0 + MW], t.sem[hs], t.sem.lsem, npid, nrid, nmask),
+                      [("mout", q0, q0 + MW)], (), 1.0, "lsem", -nne)
+            add("r", [], (), [("minb", no, no + MW)], HOP + 0.5, hs, nne, (snd,))
+
+        def step(st):
+            BK = (QB, RB)[st]
+            if st == 1:
+                add("v", lambda: v.tensor_copy(X("cf"), X("ci")), [L("ci")], [L("cf")], cv(LB))
+            for u in range(NS):
+                piece(st, u)
+            add("s", lambda: sc.activation(X("a5"), X("cf"), AF.Copy, bias=float(1 - 17 * KB), scale=5.0), [L("cf")], [L("a5")], cv(LB))
+            add("s", lambda: sc.activation(X("ax"), X("cf"), AF.Copy, bias=float(1 - 17 * KB + THR), scale=5.0), [L("cf")], [L("ax")], cv(LB))
+            add("t", lambda: te.matmul(t[RB][:, 0:LB], t.idf[:], X("a5"), True, False), [IDF, L("a5")], [ALL(RB)], ct(256))
+            add("t", [lambda k=k: te.matmul(t[RB][:, 0:LB], t.es[:, 128 * k:128 * k + 128], X("a", k, None, 128, 16), False, False) for k in range(16)],
+                [("es", 0, 2048), L("a")], [ALL(RB)], ct(1024))
+            add("t", [lambda k=k: te.matmul(t[RB][:, 0:LB], t.ew[:, 128 * k:128 * k + 128], X("m", k, None, 128, 16), False, k == 15) for k in range(16)],
+                [("ew", 0, 2048), L("m")], [ALL(RB)], ct(1024))
+
+            def qc():
+                add("t", lambda: te.matmul(t[BK][:, 128:128 + LB], t.idf[:], X("cf"), True, False), [IDF, L("cf")], [ALL(BK)], ct(256))
+
+            def qp():
+                add("t", lambda: te.matmul(t[BK][:, 128:128 + LB], t.bq[:], X("pa"), False, True), [("bq", 0, 128), L("pa")], [ALL(BK)], ct(64))
+
+            def bm():
+                add("v", lambda: v.tensor_tensor(X("bm"), X("ax"), t[RB][:, 0:LB], ALU.min), [L("ax"), ALL(RB)], [L("bm")], cv(LB))
+            if st == 0:
+                qc()
+            add("v", lambda: v.tensor_scalar(X("pa"), t[RB][:, 0:LB], float(THR - 17 * KB), None, ALU.is_ge), [ALL(RB)], [L("pa")], cv(LB))
+            if st == 0:
+                qp()
+                bm()
+            else:
+                key_and_hop()
+                bm()
+                qc()
+                qp()
+            add("v", lambda: v.tensor_tensor(X("yi"), X("bm"), t[BK][:, 128:128 + LB], ALU.min), [L("bm"), ALL(BK)], [L("yi")], cv(LB))
+            add("v", lambda: v.tensor_scalar(X("ci"), X("yi"), 4095, None, ALU.bitwise_and), [L("yi")], [L("ci")], cv(LB))
+            if st == 0:
+                add("v", lambda: v.tensor_copy(X("co"), X("ci")), [L("ci")], [L("co")], cv(LB))
+                add("t", lambda: te.matmul(t[QB][0:LB, 224:232], X("pa"), t.bo[:, 0::16], True, True), [L("pa"), BO], [ALL(QB)], ct(64))
+            else:
+                add("v", lambda: v.tensor_copy(t.cw[:, cs:ce].indirect(X("ls", 0, H)), X("ci")), [L("ci"), L("ls")], [("cw", cs, ce)], (0.05 + 3.8 * LB * CYC) * FAC)
+        step(0)
+        step(1)
+        if s == N - 1:
+            add("y", lambda: g.sync.dma_start(t.yg[:, cs:ce], t.cw[:, cs:ce]), [("cw", cs, ce)], (), 0.06, nm("oyg", b), 16, (), 4.0)
+
+    for s in range(N):
+        for b in range(NB):
+            cur[0] = BON * b
+            slice_block(s, b)
+    cur[0] = 0.0
+
+    def home(b):
+        L, X, LX, RB, QB = tiles(b)
+        o = mi(N, b)
+        L0, L1 = t[LX[0]][0:LB, 256:384], t[LX[1]][0:8, 0:LB]
+        add("s", lambda: sc.activation(X("rb", 0, LB, LB), t.e4[0:LB, :], AF.Identity, scale=t.minb[0:LB, o + LB:o + LB + 1]), [E4, ("minb", o + LB, o + LB + 8)], [L("rb")], cv(LB))
+        add("t", [lambda: te.matmul(L0, t.minb[:, o:o + LB], t.idp[:], True, False), lambda: te.matmul(L0, t.ck[:], t.idn[:], False, False),
+                  lambda: te.matmul(L0, X("rb", 0, LB, LB), t.ml[0:LB, :], False, True)],
+            [("minb", o, o + LB), ("idn", 0, 128), CK, ("idp", 0, 128), L("rb"), ML], [ALL(LX[0])], ct(1152))
+        add("v", lambda: v.tensor_copy(X("vo", 0, 128, LB), L0), [ALL(LX[0])], [L("vo")], cv(128))
+        for (q, k0) in (("y", 0), ("s", 4)):
+            add(q, [lambda k=k, q=q: eng[q].dma_start(t.yv[16 * k:16 * k + 16, LB * b:LB * b + LB], X("vo", 16 * k, 16 * k + 16, LB)) for k in range(k0, k0 + 4)],
+                [L("vo")], (), 0.24, nm("oyv", b), 64 if q == "y" else 128, (), 2.0)
+        add("t", lambda: te.matmul(L1, t.minb[0:LB, o + LB + 8:o + MW], t.idf[0:LB, 0:LB], True, True), [("minb", o + LB + 8, o + MW), IDF], [ALL(LX[1])], ct(256))
+        add("s", lambda: sc.activation(X("yo", 0, LB, 8), L1, AF.Copy), [ALL(LX[1])], [L("yo")], cv(64))
+        add("y", lambda: g.sync.dma_start(t.ym[:, LB * b:LB * b + LB], X("yo", 0, LB, 8)), [L("yo")], (), 0.06, nm("oym", b), 16, (), 2.0)
+    for b in range(NB):
+        home(b)
+
+    order = schedule(nodes)
+    pos = {i: k for k, i in enumerate(order)}
+    cnt, known, tok, total = {}, {q: {} for q in eng}, {}, {}
+    for i in order:
+        d = nodes[i]
+        q = d["q"]
+        if q == "r":
+            tok[i] = (d["sem"], d["val"], {})
+            total[d["sem"]] = d["val"]
+            continue
+        kn = known[q]
+        for j in sorted(d["dep"], key=lambda j: -pos[j]):
+            if not d["dep"][j]:
+                continue
+            sem, val, jk = tok[j]
+            if kn.get(sem, 0) >= val:
+                continue
+            eng[q].wait_ge(t.sem[sem], val)
+            for (a, w) in list(jk.items()) + [(sem, val)]:
+                kn[a] = max(kn.get(a, 0), w)
+        ins = None
+        for f in d["f"]:
+            ins = f()
+            if d["sem"] and d["val"] > 0:
+                ins.then_inc(t.sem[d["sem"]], 16)
+        if d["sem"] is None:
+            sem = csem[q]
+            cnt[sem] = cnt.get(sem, 0) + 1
+            ins.then_inc(t.sem[sem], 1)
+            tok[i] = (sem, cnt[sem], dict(kn))
+            total[sem] = cnt[sem]
+        elif d["val"] > 0:
+            tok[i] = (d["sem"], d["val"], dict(kn))
+            total[d["sem"]] = max(d["val"], total.get(d["sem"], 0))
+        else:
+            total[d["sem"]] = total.get(d["sem"], 0) - d["val"]
+    for sem in total:
+        if known["g"].get(sem, 0) < total[sem]:
+            g.wait_ge(t.sem[sem], total[sem])

@@ -3,112 +3,100 @@ from concourse.mybir import AluOpType as ALU, AxisListType, ActivationFunctionTy
 
 N, NB = 8, 2
 LB = 128 // NB
-H = LB // 16
-LS = 16
-NS = LB // LS
-CB, CS = 16 * LB, 16 * LS
-MW = LB + 16
-GS = ((1, NS - 1),)
-BON, LOOK, HOLD = 3.0, 0.1, 0.4
-KB = 1 << 19
-W15 = 1 << 15
-THR = 10 * W15
-
-SCRATCH = {
-    "xw": ("sbuf", [128, 4096], "bfloat16"), "pw": ("sbuf", [128, 2048], "bfloat16"),
-    "pgi": ("sbuf", [128, 2048], "int32"), "cw": ("sbuf", [128, 2048], "float32"),
-    "vt": ("sbuf", [128, 128], "int32"), "vtb": ("sbuf", [128, 128], "bfloat16"),
-    "limo": ("sbuf", [128, 128], "bfloat16"), "limt": ("sbuf", [128, 128 * N], "bfloat16"),
-    "minb": ("sbuf", [128, MW * NB * (N + 1)], "float32"), "mout": ("sbuf", [128, MW * NB * N], "float32"),
-    "mia": ("sbuf", [128, 8 * NB * N], "int32"), "mxo": ("sbuf", [128, 8 * NB * N], "int32"),
-    "onef": ("sbuf", [128, 128], "float32"), "oneb": ("sbuf", [128, 128], "bfloat16"), "posb": ("sbuf", [128, 128], "bfloat16"),
-    "bias": ("sbuf", [128, 1], "float32"),
-    "idf": ("sbuf", [128, 128], "float32"), "idb": ("sbuf", [128, 128], "bfloat16"), "nid": ("sbuf", [128, 128], "bfloat16"),
-    "idp": ("sbuf", [128, 128], "float32"), "idn": ("sbuf", [128, 128], "float32"),
-    "bo0": ("sbuf", [128, 128], "bfloat16"), "bo": ("sbuf", [128, 128], "bfloat16"),
-    "bq1": ("sbuf", [128, 128], "float32"), "bq2": ("sbuf", [128, 128], "float32"), "bq": ("sbuf", [128, 128], "bfloat16"),
-    "pmt": ("sbuf", [128, 128], "bfloat16"), "es": ("sbuf", [128, 2048], "bfloat16"), "ew": ("sbuf", [128, 2048], "bfloat16"),
-    "ex": ("sbuf", [128, 2048], "bfloat16"),
-    "ix": ("sbuf", [128, 128], "int32"), "ix2": ("sbuf", [128, 128], "int32"), "ml": ("sbuf", [128, 128], "bfloat16"),
-    "ka": ("sbuf", [128, LB], "int32"), "ka2": ("sbuf", [128, LB], "int32"), "kb": ("sbuf", [128, LB], "int32"), "ck": ("sbuf", [128, LB], "float32"),
-    "r16": ("sbuf", [128, LB], "bfloat16"), "cli": ("sbuf", [128, H], "int32"), "cli2": ("sbuf", [128, H], "int32"), "cl": ("sbuf", [128, H], "uint16"),
-    "e4a": ("sbuf", [128, LB], "bfloat16"), "e4": ("sbuf", [128, LB], "bfloat16"), "e4s": ("sbuf", [128, LB], "bfloat16"), "e4n": ("sbuf", [128, LB], "bfloat16"),
+H, CB, MW = LB // 16, 16 * LB, LB + 8
+CUTS = ((16, 18), (20, 20))
+FIRST, PERIOD = 10.0, 16.365
+TABLE = {
+    (0, 0, "v"): "co1@0.00 f1@0.37 po1@0.83 f2@0.88 gq1@1.27 gq2@1.66 m1@2.63 m2@2.84 m3@3.07 m4@3.49 kc1@3.71 yi1@4.59 pa1@4.64 se1@4.69 ci1@4.87 cf1@5.23 co2@5.52 kc2@7.44 li1@7.83 eout1@8.28 lz1@8.58",
+    (0, 0, "s"): "pg_1@0.17 ax1@0.31 f1@0.45 f2@0.83 gq1@1.22 gq2@1.67 a1@2.18 a2@2.39 a3@2.62 a4@2.84 fq1@3.05 cx1@3.10",
+    (0, 0, "t"): "P71@-1.84 P61@-1.74 P51@-1.63 P41@-1.40 Q1@0.54 R1@1.00 P52@1.13 P42@1.23 P62@1.45 P72@1.56 P43@1.84 P53@1.94 P63@2.29 P73@2.39 Q2@3.34 R2@3.47 R3@3.94 Q3@4.93 R4@5.07 Q4@5.68",
+    (0, 0, "g"): "eout1@8.57",
+    (0, 1, "v"): "f1@5.88 f2@6.65 gq1@7.49 gq2@7.94 m1@8.93 m2@9.19 m3@9.48 m4@9.71 pa1@10.80 bm1@11.21 pr1@11.40 mk1@11.46 rb1@11.69 mxo1@12.24 f81@12.29 w1@13.28 yi1@13.34 ci1@13.62 cw1@14.21",
+    (0, 1, "s"): "f1@6.13 f2@6.99 gq1@7.42 gq2@8.03 a1@8.48 ax1@8.69 a2@8.75 a3@9.03 a4@9.27 pc1@12.83 mout1@14.57 fout1@14.57 cc1@14.70",
+    (0, 1, "t"): "P41@6.67 P51@6.88 P42@6.98 P52@7.09 P61@7.63 P43@8.14 P53@8.25 P71@8.48 P62@8.58 P63@8.70 P72@8.83 P73@8.93 R1@9.03 R2@9.74 R3@10.16 Q1@11.09 Q2@11.12 Q3@11.80 Q4@11.98 R4@12.11 Q5@12.58 Q6@12.69 Q7@13.93 Q8@14.08",
+    (0, 1, "g"): "mxo1@12.53 mout1@14.87 fout1@14.87",
+    (1, 0, "v"): "co1@3.36 f1@3.76 po1@4.16 f2@4.21 gq1@4.93 gq2@5.57 m1@6.22 m2@6.43 m3@7.01 m4@7.22 kc1@7.89 se1@8.34 pa1@8.48 yi1@8.53 ci1@8.82 cf1@9.14 co2@9.43 kc2@9.93 li1@10.59 eout1@11.16 lz1@11.27",
+    (1, 0, "s"): "ax1@3.36 pg_1@3.49 f1@3.73 f2@4.20 gq1@4.67 gq2@5.14 a1@5.71 a2@5.92 a3@6.56 a4@6.78 cx1@7.84 fq1@7.98",
+    (1, 0, "t"): "Q1@3.88 P41@4.35 P61@4.45 P71@4.56 P51@4.66 P42@4.76 P52@4.95 P43@5.37 P53@5.47 P72@5.58 P62@5.71 P63@5.84 P73@6.11 R1@6.21 R2@7.22 R3@7.73 Q2@8.35 Q3@8.80 R4@9.16 Q4@9.48",
+    (1, 0, "g"): "eout1@11.45",
+    (1, 1, "v"): "f1@9.98 f2@10.28 gq1@10.86 gq2@11.75 m1@12.35 m2@12.56 m3@12.79 m4@13.07 pa1@14.16 bm1@14.47 pr1@14.76 mk1@14.81 rb1@15.05 yi1@15.20 ci1@15.48 mxo1@15.60 f81@15.65 cw1@15.77 w1@16.50",
+    (1, 1, "s"): "ax1@9.48 f1@9.72 f2@10.19 gq1@10.66 gq2@11.13 a1@11.71 a2@11.92 a3@12.34 a4@12.62 pc1@15.28 cc1@16.26 fout1@17 mout1@17.97",
+    (1, 1, "t"): "P41@9.38 P51@9.64 P52@10.57 P71@10.67 R1@10.77 P61@10.90 P72@11.17 P42@11.27 P43@11.37 P53@11.48 P62@11.58 P63@12.01 P73@12.28 R2@13.07 R3@13.52 Q1@14.45 Q2@14.48 R4@14.83 Q3@15.16 Q4@15.34 Q5@15.94 Q6@16.04 Q7@16.96 Q8@17.11",
+    (1, 1, "g"): "mxo1@15.89 fout1@17.3 mout1@18.27",
 }
-TILE = {"f": (CB, "bfloat16"), "gq": (CB, "bfloat16"), "a": (CB, "bfloat16"), "m": (CB, "bfloat16"), "li": (4, "int32"), "ls": (4, "uint16"),
-        "cf": (LB, "float32"), "co": (LB, "uint16"), "lk": (4, "float32"), "mo": (4, "float32"), "pg_": (LB, "bfloat16"), "po": (LB, "uint16"),
-        "a5": (LB, "float32"), "ax": (LB, "float32"), "pa": (LB, "bfloat16"), "bm": (LB, "float32"), "yi": (LB, "int32"), "ci": (LB, "int32"),
-        "f8": (16, "bfloat16"), "mm": (4, "float32"), "mn": (4, "int32"), "od": (4, "int32"), "rb": (LB, "bfloat16"), "mk": (128, "bfloat16"),
-        "ns": (LB, "float32"), "se": (LB, "float32"), "ua": (LB, "float32"), "vo": (128, "float32"), "yo": (LB, "float32")}
-for _n in TILE:
-    SCRATCH[_n] = ("sbuf", [128, NB * TILE[_n][0]], TILE[_n][1])
+START = {(0, 0, "s"): "pg_1@.8", (0, 0, "v"): "ax1@.15 cx1@.2", (1, 0, "v"): "ax1@4.3 po1@4.75 cx1@5.3", (1, 0, "s"): "pg_1@4.1",
+         (0, -1, "v"): "xw1@.5 xw2@.6 xw3@.7 xw4@2.05 cw5@13.4 cw6@13.7 cw7@14.3 cw8@14.6", (0, 0, "t"): "Q1@1.3"}
+END = {(0, 1, "t"): "R4@11.3 R5@12 R6@14.55 Q5@14.1", (0, 1, "v"): "yi1@14.95 ci1@15.3 cw1@15.7", (1, 1, "t"): "R4@14.6 Q3@14.9 Q4@15 R5@15.3 Q5@15.9 R6@16", (1, 1, "v"): "f81@14.9 w1@15.6 yi1@16.3 ci1@16.6 cw1@16.9"}
+KB = 1 << 20
+WT = 1 << 16
+THR = 10 * WT
+OFF = -33 * KB // 32
+FQ = 151
+KF = 2 * (4096 * (FQ + 1) - OFF - THR)
+NEW = 15872 - 1024
+BIG = 65536.0
+ZS = 1.0 / (1 << 17)
+MAGIC = 1.5 * (1 << 23)
+
+SCRATCH = {"xw": ("sbuf", [128, 8192], "bfloat16"), "pw": ("sbuf", [128, 2048], "bfloat16"), "pgi": ("sbuf", [128, 2048], "int32"),
+           "cw": ("sbuf", [128, 2048], "float32"), "es": ("sbuf", [128, 2048], "bfloat16"), "ex": ("sbuf", [128, 2048], "bfloat16"),
+           "limt": ("sbuf", [128, 128 * N], "bfloat16"), "minb": ("sbuf", [128, MW * NB * N], "float32"), "mout": ("sbuf", [128, MW * NB * N], "float32"),
+           "fin": ("sbuf", [128, MW * NB], "bfloat16"), "fout": ("sbuf", [128, MW * NB], "bfloat16")}
+for _w, _d, _names in ((8 * NB * N, "uint16", "mia mxo ein eout"), (128, "int32", "vt ix ix2"), (128, "float32", "onef idf idn idz bq1 bq2"),
+                       (128, "bfloat16", "vtb limo oneb posb thb idb nid nbig n4k bo0 bo bq bk pmt ml mlp mln mlz"), (LB, "int32", "ka ka2 kb"),
+                       (LB, "float32", "ck ck2 sm"), (LB, "bfloat16", "r16 e4a e4 e4n e4z"), (H, "int32", "cli"), (H, "uint16", "cl"), (H, "bfloat16", "cz cy")):
+    for _n in _names.split():
+        SCRATCH[_n] = ("sbuf", [128, _w], _d)
+TILE = {}
+for _w, _d, _names in ((CB, "bfloat16", "f gq a m"), (2 * LB, "float32", "cc vo"), (2 * LB, "bfloat16", "pc mk"), (2 * LB, "int32", "kc"), (LB, "uint16", "co po"),
+                       (LB, "float32", "cf ax cx bm w yo"), (LB, "bfloat16", "pg_ fq pa rb se"), (LB, "int32", "yi ci"), (16, "bfloat16", "f8"), (8, "int32", "li"), (4, "float32", "lz pr")):
+    for _n in _names.split():
+        TILE[_n] = _w
+        SCRATCH[_n] = ("sbuf", [128, NB * _w], _d)
 for _b in range(8):
     SCRATCH["pb%d" % _b] = ("psum", [128, 512], "float32")
 
-SEMAPHORES = ["qv", "qs", "qt", "qg", "lsem", "limr", "dlim", "dvv", "dxt"]
+SEMAPHORES = ["qv", "qs", "qt", "qg", "lsem", "limr", "dlim", "dvvy", "dvvs", "dxt"]
 SEMAPHORES += ["%s%d" % (n, b) for n in ("dpg", "dpre", "oyg", "oyv", "oym") for b in range(NB)]
-SEMAPHORES += ["h%d_%d" % (s, b) for s in range(1, N + 1) for b in range(NB)] + ["k%d_%d" % (s, b) for s in range(1, N) for b in range(NB)]
+SEMAPHORES += ["h%d_%d" % (s, b) for s in range(1, N + 1) for b in range(NB)] + ["%s%d_%d" % (n, s, b) for n in "ke" for s in range(1, N) for b in range(NB)]
 
-CYC, FAC, WAKE, XG, PEC, HOP = 0.00083, 1.0, 0.2, 1.56, 0.0004, 4.0
+CYC, WAKE, XG, PEC, HOP = 0.00083, 0.2, 1.56, 0.0004, 4.0
 
 
 def cv(n):
-    return max(64, n) * CYC * FAC
+    return max(64, n) * CYC
 
 
 def cg(n):
-    return (0.055 + XG * n * CYC) * FAC
-
-
-def ct(n):
-    return n * PEC
+    return 0.055 + XG * n * CYC
 
 
 def schedule(nodes):
     n = len(nodes)
-    succ = [[] for _ in range(n)]
-    for i, d in enumerate(nodes):
-        for j in d["dep"]:
-            succ[j].append(i)
-    pri = [0.0] * n
+    pred = [[(j, nodes[j]["lat"] + WAKE if need else WAKE * (nodes[j]["q"] == "r")) for j, need in d["dep"].items()] for d in nodes]
+    path, key, busy = [d["c"] + d["lat"] for d in nodes], [0.0] * n, {}
     for i in range(n - 1, -1, -1):
+        for j, w in pred[i]:
+            path[j] = max(path[j], nodes[j]["c"] + w + path[i])
+    read = lambda table: {k + (w.split("@")[0],): float(w.split("@")[1]) for k in table for w in table[k].split()}
+    table, ends = read(TABLE), {0: read(START), N - 1: read(END)}
+    for i in sorted(range(n), key=lambda i: -path[i]):
         d = nodes[i]
-        pri[i] = d["c"] + d["lat"] + WAKE + max([pri[k] for k in succ[i]] + [0.0])
+        s, name = d["turn"] // NB, (d["turn"] % NB, d["step"], d["q"], d["name"])
+        if d["step"] >= 0 or name in ends[0]:
+            key[i] = FIRST + PERIOD * s + ends.get(s, {}).get(name, table.get(name, 0.0))
+        elif s > 0:
+            key[i] = FIRST + PERIOD * s
+        else:
+            t, line = max([0.0] + [key[j] + nodes[j]["c"] + w for j, w in pred[i]]), busy.setdefault(d["q"] if d["q"] != "r" else i, [])
+            for (a, e) in sorted(line):
+                if a < t + d["c"] and t < e:
+                    t = e
+            line.append((t, t + d["c"]))
+            key[i] = t
     for i in range(n):
-        pri[i] -= nodes[i]["bl"]
-    left = [len(d["dep"]) for d in nodes]
-    ready = [0.0] * n
-    free = {"v": 0.0, "s": 0.0, "t": 0.0, "g": 0.0, "y": 0.0}
-    pool = {q: [] for q in list(free) + ["r"]}
-    for i in range(n):
-        if left[i] == 0:
-            pool[nodes[i]["q"]].append(i)
-    order = []
-    while len(order) < n:
-        best = None
-        for q in pool:
-            if not pool[q]:
-                continue
-            f = free.get(q, 0.0)
-            t0 = min(max(f, ready[i]) for i in pool[q])
-            i = max((i for i in pool[q] if max(f, ready[i]) <= t0 + LOOK), key=lambda i: pri[i])
-            e0 = max(f, ready[i]) + HOLD * nodes[i]["c"]
-            i = max((j for j in pool[q] if ready[j] <= e0), key=lambda j: pri[j])
-            st = max(f, ready[i])
-            if best is None or st < best[0]:
-                best = (st, q, i)
-        st, q, i = best
-        pool[q].remove(i)
-        en = st + nodes[i]["c"]
-        if q != "r":
-            free[q] = en
-        order.append(i)
-        for k in succ[i]:
-            w = 0.0 if (nodes[k]["q"] == q and not nodes[k]["dep"][i]) else WAKE
-            ready[k] = max(ready[k], en + nodes[i]["lat"] + w)
-            left[k] -= 1
-            if left[k] == 0:
-                pool[nodes[k]["q"]].append(k)
-    return order
+        key[i] = max([key[i]] + [key[j] + 1e-7 for j, w in pred[i]])
+    return sorted(range(n), key=lambda i: key[i])
 
 
 def rank_program(g, core, T, topo):
@@ -117,8 +105,9 @@ def rank_program(g, core, T, topo):
         return
     eng = {"v": g.vector, "s": g.scalar, "t": g.tensor, "g": g, "y": g.sync}
     csem = {"v": "qv", "s": "qs", "t": "qt", "g": "qg"}
-    nodes, last, cur = [], {}, [0.0]
-    STREAM = ("ls", "co", "po", "cw", "f")
+    nodes, last, cur = [], {}, [0, -1, {}]
+    ROLE = {"pb%d" % k: "RQ"[k % 2] if k < 2 * NB else "P%d" % k for k in range(8)}
+    STREAM = ("co", "po", "cw", "f", "kc", "cc", "pc", "eout")
 
     def add(q, fns, R=(), W=(), c=0.08, sem=None, val=None, after=(), lat=0.0):
         i = len(nodes)
@@ -143,72 +132,79 @@ def rank_program(g, core, T, topo):
                 rec.append((i, a, b, wr))
         for j in after:
             dep[j] = dep.get(j, False)
-        nodes.append({"q": q, "f": fns if isinstance(fns, list) else [fns], "dep": dep, "c": c, "sem": sem, "val": val, "lat": lat, "bl": cur[0]})
+        name = (list(W) + list(R))[0][0]
+        name = ROLE.get(name, name)
+        seen = cur[2][q, name] = cur[2].get((q, name), 0) + 1
+        nodes.append({"q": q, "f": fns if isinstance(fns, list) else [fns], "dep": dep, "c": c, "sem": sem, "val": val, "lat": lat,
+                      "turn": cur[0], "step": cur[1], "name": name + str(seen)})
         return i
 
     t = T
     nm = lambda n, b: "%s%d" % (n, b)
     v, sc, te = g.vector, g.scalar, g.tensor
-    IDF, CK, IDB, NID, BO, ML, E4 = ("idf", 0, 128), ("ck", 0, LB), ("idb", 0, 128), ("nid", 0, 128), ("bo", 0, 128), ("ml", 0, 128), ("e4", 0, LB)
+    C = lambda n: (n, 0, SCRATCH[n][1][1])
+    ALL = lambda bank: (bank, 0, 512)
+    BANK = [("pb%d" % (2 * b), "pb%d" % (2 * b + 1)) for b in range(NB)]
+
+    def mm(bank, c0, terms, p=128, start=True, stop=True):
+        fns, R, c = [], [], 0.0
+        for k, (l, r, n, f32, rd) in enumerate(terms):
+            fns.append(lambda l=l, r=r, n=n, k=k: te.matmul(t[bank][0:p, c0:c0 + n], l, r, start and k == 0, stop and k == len(terms) - 1))
+            R += rd
+            c += max(min(64, p), n) * (4 if f32 else 1) * PEC
+        return add("t", fns, R, [ALL(bank)], c)
+
+    prev = {"y": (), "s": ()}
 
     def load(fns, W, sem, cost, q="y"):
-        add(q, fns, (), W, 0.06 * len(fns), sem, 16 * len(fns), (), cost)
-    load([lambda k=k: g.scalar.dma_start(t.vt[:, 16 * k:16 * k + 16], t.vv[16 * k:16 * k + 16, :]) for k in range(8)], [("vt", 0, 128)], "dvv", 3.0, "s")
-    load([lambda: g.sync.dma_start(t.limo[:], t.lim[:])], [("limo", 0, 128)], "dlim", 2.5)
+        prev[q] = (add(q, fns, (), W, 0.06 * len(fns), sem, 16 * len(fns), prev[q], cost),)
+    for (q, k0) in (("y", 0), ("s", 4)):
+        load([lambda k=k, q=q: eng[q].dma_start(t.vt[:, 16 * k:16 * k + 16], t.vv[16 * k:16 * k + 16, :]) for k in range(k0, k0 + 4)], [("vt", 16 * k0, 16 * k0 + 64)], "dvv" + q, 2.5, q)
+    load([lambda: g.scalar.dma_start(t.limo[:], t.lim[:])], [C("limo")], "dlim", 2.5, "s")
     for b in range(NB):
-        load([lambda b=b: g.sync.dma_start(t.pgi[:, CB * b:CB * b + CB], t.pg[:, CB * b:CB * b + CB])], [("pgi", CB * b, CB * b + CB)], nm("dpg", b), 4.5 + 5.5 * b)
+        cs, ce = CB * b, CB * b + CB
+        load([lambda cs=cs, ce=ce: g.sync.dma_start(t.pgi[:, cs:ce], t.pg[:, cs:ce])], [("pgi", cs, ce)], nm("dpg", b), 4.6 + 8.8 * b)
         if b == 0:
-            load([lambda: g.sync.dma_start(t.xw[:], t.xt[:])], [("xw", 0, 4096)], "dxt", 7.0)
-        load([lambda b=b: g.sync.dma_start(t.pw[:, CB * b:CB * b + CB], t.pre[:, CB * b:CB * b + CB])], [("pw", CB * b, CB * b + CB)], nm("dpre", b), 7.5 + 4.0 * b)
+            load([lambda: g.sync.dma_start(t.xw[:, 0:4096], t.xt[:])], [("xw", 0, 4096)], "dxt", 9.6)
+        load([lambda cs=cs, ce=ce: g.sync.dma_start(t.pw[:, cs:ce], t.pre[:, cs:ce])], [("pw", cs, ce)], nm("dpre", b), 10.8 + 3.9 * b)
 
     def vmem(buf, a, b, val):
         add("v", lambda: v.memset(t[buf][:, a:b], val), (), [(buf, a, b)], cv((b - a) * (0.5 if SCRATCH[buf][2] == "bfloat16" else 1)))
 
-    def vts(out, in0, n, fn, half=False):
-        add("v", fn, [(in0, 0, n)], [(out, 0, n)], cv(n * (0.5 if half else 1)))
+    def vts(out, in0, s1, op=ALU.mult):
+        add("v", lambda: v.tensor_scalar(t[out][:], t[in0][:], s1, None, op), [C(in0)], [C(out)], cv(C(out)[2]))
 
-    def gen(out, n, fn, in_=None):
-        add("g", fn, [(in_, 0, n)] if in_ else (), [(out, 0, n)], (0.17 + 2 * n * CYC) * FAC)
-    vmem("onef", 0, 128, 1.0)
-    vmem("oneb", 0, 128, 1.0)
-    vmem("posb", 0, 128, 1024.0)
-    vmem("bias", 0, 1, -15.0)
-    gen("idf", 128, lambda: g.affine_select(t.idf[:], t.onef[:], [[-1, 128]], ALU.is_equal, 0.0, 0, 1), "onef")
-    gen("pmt", 128, lambda: g.affine_select(t.pmt[:], t.posb[:], [[-H, NB], [-8, 16], [-1, H]], ALU.is_equal, 0.0, 0, 1), "posb")
-    gen("ka", LB, lambda: g.iota(t.ka[:], [[0, LB]], 0, 16))
-    gen("kb", LB, lambda: g.iota(t.kb[:], [[-1, 16], [-256, H]], 65536 + 1023, 0))
-    gen("cli", H, lambda: g.iota(t.cli[:], [[0, H]], 0, 1))
-    gen("r16", LB, lambda: g.iota(t.r16[:], [[0, NS], [16, LS]], 0, 0, allow_small_or_imprecise_dtypes=True))
-    gen("bo0", 128, lambda: g.affine_select(t.bo0[:], t.oneb[:], [[-16, 8], [0, 16]], ALU.is_ge, 0.0, 0, 1), "oneb")
-    gen("bo", 128, lambda: g.affine_select(t.bo[:], t.bo0[:], [[16, 8], [0, 16]], ALU.is_ge, 0.0, 15, -1), "bo0")
-    gen("es", 2048, lambda: g.iota(t.es[:], [[0, 2048]], 0, 0, allow_small_or_imprecise_dtypes=True))
-    gen("ix", 128, lambda: g.iota(t.ix[:], [[-1, 128]], 128, 1))
-    gen("e4a", LB, lambda: g.affine_select(t.e4a[:], t.oneb[:, 0:LB], [[0, 16], [-16, H]], ALU.is_ge, 0.0, 0, 1), "oneb")
-    gen("e4", LB, lambda: g.affine_select(t.e4[:], t.e4a[:], [[0, 16], [16, H]], ALU.is_ge, 0.0, 15, -1), "e4a")
-    gen("mout", MW * NB * N, lambda: g.iota(t.mout[:], [[0, MW * NB * N]], 0, 0, allow_small_or_imprecise_dtypes=True))
-    vts("idb", "idf", 128, lambda: v.tensor_copy(t.idb[:], t.idf[:]))
-    add("v", lambda: v.tensor_copy(t.vtb[:], t.vt[:]), [("vt", 0, 128)], [("vtb", 0, 128)], cv(128))
-    vts("ka2", "ka", LB, lambda: v.tensor_scalar(t.ka2[:], t.ka[:], 255, None, ALU.bitwise_and))
-    add("v", lambda: v.tensor_tensor(t.ck[:], t.kb[:], t.ka2[:], ALU.subtract), [("ka2", 0, LB), ("kb", 0, LB)], [CK], cv(2 * LB))
-    vts("cli2", "cli", H, lambda: v.tensor_scalar(t.cli2[:], t.cli[:], H - 1, None, ALU.bitwise_and))
-    vts("cl", "cli2", H, lambda: v.tensor_copy(t.cl[:], t.cli2[:]))
+    def gen(out, fn, in_=None):
+        add("g", fn, [C(in_)] if in_ else (), [C(out)], 0.17 + 2 * C(out)[2] * CYC)
+    for (buf, val) in (("onef", 1.0), ("oneb", 1.0), ("posb", 1024.0), ("thb", float(-THR)), ("es", 0.0), ("sm", 1.0), ("cy", 0.5 + NEW * ZS)):
+        vmem(buf, 0, C(buf)[2], val)
+    add("v", lambda: v.memset(t.sm[:, 0::16], 0.0), (), [C("sm")], cv(1))
+    gen("idf", lambda: g.affine_select(t.idf[:], t.onef[:], [[-1, 128]], ALU.is_equal, 0.0, 0, 1), "onef")
+    gen("pmt", lambda: g.affine_select(t.pmt[:], t.posb[:], [[-1, 8], [-8, 16]], ALU.is_equal, 0.0, 0, 1), "posb")
+    gen("ka", lambda: g.iota(t.ka[:], [[0, LB]], 0, 16))
+    gen("kb", lambda: g.iota(t.kb[:], [[-256, H], [-1, 16]], 1023, 0))
+    gen("cli", lambda: g.iota(t.cli[:], [[16, H]], 15, 0))
+    gen("r16", lambda: g.iota(t.r16[:], [[16, LB]], 0, 0, allow_small_or_imprecise_dtypes=True))
+    gen("bo0", lambda: g.affine_select(t.bo0[:], t.oneb[:], [[-16, 8], [0, 16]], ALU.is_ge, 0.0, 0, 1), "oneb")
+    gen("bo", lambda: g.affine_select(t.bo[:], t.bo0[:], [[16, 8], [0, 16]], ALU.is_ge, 0.0, 15, -1), "bo0")
+    gen("ix", lambda: g.iota(t.ix[:], [[-1, 128]], 128, 1))
+    gen("e4a", lambda: g.affine_select(t.e4a[:], t.oneb[:, 0:LB], [[-16, H], [0, 16]], ALU.is_ge, 0.0, 0, 1), "oneb")
+    gen("e4", lambda: g.affine_select(t.e4[:], t.e4a[:], [[16, H], [0, 16]], ALU.is_ge, 0.0, 15, -1), "e4a")
+    add("v", lambda: v.tensor_copy(t.idb[:], t.idf[:]), [C("idf")], [C("idb")], cv(128))
+    add("v", lambda: v.tensor_copy(t.vtb[:], t.vt[:]), [C("vt")], [C("vtb")], cv(128))
+    vts("ka2", "ka", 255, ALU.bitwise_and)
+    add("v", lambda: v.tensor_tensor(t.ck[:], t.kb[:], t.ka2[:], ALU.subtract), [C("ka2"), C("kb")], [C("ck")], cv(2 * LB))
+    vts("ck2", "ck", float(NEW), ALU.add)
+    add("v", lambda: v.tensor_copy(t.cl[:], t.cli[:]), [C("cli")], [C("cl")], cv(1))
+    for k in range(0, 2048, 256):
+        add("v", lambda k=k: v.tensor_copy(t.cw[:, k:k + 256], t.pgi[:, k:k + 256]), [("pgi", k, k + 256)], [("cw", k, k + 256)], cv(256))
     for b in range(NB):
-        add("v", lambda b=b: v.tensor_copy(t.cw[:, CB * b:CB * b + CB], t.pgi[:, CB * b:CB * b + CB]), [("pgi", CB * b, CB * b + CB)], [("cw", CB * b, CB * b + CB)], cv(CB))
-
-    def mi(s, b):
-        return MW * (NB * s + b)
-    for b in range(NB):
-        o = mi(0, b)
-        pb = nm("pb", 6 + b)
-        add("t", [lambda b=b, pb=pb: te.matmul(t[pb][:, 448:448 + LB], t.vtb[:], t.pmt[:, LB * b:LB * b + LB], True, True)],
-            [("vtb", 0, 128), ("pmt", 0, 128)], [(pb, 0, 512)], ct(64))
-        add("v", lambda o=o, pb=pb: v.tensor_tensor(t.minb[:, o:o + LB], t.ck[:], t[pb][:, 448:448 + LB], ALU.add), [(pb, 0, 512), CK], [("minb", o, o + LB)], cv(LB))
+        o, QB = MW * b, BANK[b][1]
+        mm(QB, 448, [(t.vtb[:], t.pmt[:, LB * b:LB * b + LB], LB, False, [C("vtb"), C("pmt")])])
+        add("v", lambda o=o, QB=QB: v.tensor_tensor(t.minb[:, o:o + LB], t.ck[:], t[QB][:, 448:448 + LB], ALU.add), [ALL(QB), C("ck")], [("minb", o, o + LB)], cv(LB))
         vmem("minb", o + LB, o + MW, 0.0)
-        for j in range(H):
-            add("v", lambda j=j, b=b, o=o: v.tensor_reduce(t.mia[:, 8 * b + j:8 * b + j + 1], t.minb[:, o + j:o + LB:H], AxisListType.X, ALU.max),
-                [("minb", o, o + LB)], [("mia", 8 * b + j, 8 * b + j + 1)], cv(16))
-    add("t", lambda: te.matmul(t.pb0[:, 0:128], t.limo[:], t.idb[:], True, True), [("limo", 0, 128), IDB], [("pb0", 0, 512)], ct(128))
-    add("s", lambda: sc.activation(t.limt[:, 0:128], t.pb0[:, 0:128], AF.Copy), [("pb0", 0, 512)], [("limt", 0, 128)], cv(128))
+    mm("pb0", 0, [(t.limo[:], t.idb[:], 128, False, [C("limo"), C("idb")])])
+    add("s", lambda: sc.activation(t.limt[:, 0:128], t.pb0[:, 0:128], AF.Copy), [ALL("pb0")], [("limt", 0, 128)], cv(128))
     nxt = T.cores[(rank + 1) % N]
     nrid, npid, _ = topo.addr(nxt)
     nmask = topo.mask(core, nxt)
@@ -223,178 +219,212 @@ def rank_program(g, core, T, topo):
     ne = bin(mask).count("1")
     limsend = add("g", lambda: g.remote_dma_fused([RemoteDMATransfer(dst_ids=dst, dma_engine_mask=mask, remote_sem=t.sem.limr,
                   srcs=[t.limt[:, 0:128]], dsts=dsts)], local_sem=t.sem.lsem), [("limt", 0, 128)], (), 2.0, "lsem", -ne)
-    add("r", [], (), [("limt", 128, 128 * N)], 4.0, "limr", 7 * ne, (limsend,))
+    add("r", [], (), [("limt", 128, 128 * N)], 4.0, "limr", (N - 1) * ne, (limsend,))
 
+    add("s", [lambda k=k: sc.activation(t.ex[:, k::16], t.idb[:], AF.Copy, scale=1.0 / WT) for k in range(16)], [C("idb")], [C("ex")], 16 * cv(128))
     for k in range(16):
-        add("s", lambda k=k: sc.activation(t.ex[:, k::16], t.idb[:], AF.Copy), [IDB], [("ex", 0, 2048)], cv(128))
-    for k in range(16):
-        add("v", lambda k=k: v.tensor_copy(t.es[:, 128 * k + k:128 * k + 128:16], t.bo[:, k::16]), [BO], [("es", 128 * k, 128 * k + 128)], cv(8))
-    add("v", lambda: v.tensor_scalar(t.ew[:], t.es[:], float(W15), None, ALU.mult), [("es", 0, 2048)], [("ew", 0, 2048)], cv(1024))
-    vts("bq1", "idb", 128, lambda: v.tensor_scalar(t.bq1[:], t.idb[:], float(-32 * KB), None, ALU.mult))
-    vts("bq2", "bo", 128, lambda: v.tensor_scalar(t.bq2[:], t.bo[:], float(KB), None, ALU.mult))
-    add("v", lambda: v.tensor_tensor(t.bq[:], t.bq1[:], t.bq2[:], ALU.add), [("bq1", 0, 128), ("bq2", 0, 128)], [("bq", 0, 128)], cv(256))
-    vts("nid", "idb", 128, lambda: v.tensor_scalar(t.nid[:], t.idb[:], -1.0, None, ALU.mult), True)
-    vts("ix2", "ix", 128, lambda: v.tensor_scalar(t.ix2[:], t.ix[:], 15, None, ALU.bitwise_and))
-    vts("ml", "ix2", 128, lambda: v.tensor_scalar(t.ml[:], t.ix2[:], 0.0, None, ALU.is_equal))
-    vts("e4s", "e4", LB, lambda: v.tensor_scalar(t.e4s[:], t.e4[:], -1024.0, None, ALU.mult), True)
-    vts("e4n", "e4", LB, lambda: v.tensor_scalar(t.e4n[:], t.e4[:], 1024.0, None, ALU.mult), True)
-    vts("idp", "idf", 128, lambda: v.tensor_scalar(t.idp[:], t.idf[:], 1.0 / 1024, None, ALU.mult))
-    vts("idn", "idf", 128, lambda: v.tensor_scalar(t.idn[:], t.idf[:], -1.0 / 1024, None, ALU.mult))
+        add("v", lambda k=k: v.tensor_scalar(t.es[:, 128 * k + k:128 * k + 128:16], t.bo[:, k::16], float(WT), None, ALU.mult), [C("bo")], [("es", 128 * k, 128 * k + 128)], cv(8))
+    for k in range(0, 4096, 1024):
+        add("v", lambda k=k: v.tensor_copy(t.xw[:, 4096 + k:5120 + k], t.xw[:, k:k + 1024]), [("xw", k, k + 1024)], [("xw", 4096 + k, 5120 + k)], cv(512))
+    vts("ix2", "ix", 15, ALU.bitwise_and)
+    vts("ml", "ix2", 0.0, ALU.is_equal)
+    for (out, in0, f) in (("bk", "bo", KF), ("n4k", "idb", -4096), ("bq1", "idb", -17 * KB), ("bq2", "bo", KB), ("nid", "idb", -1), ("nbig", "idb", -BIG), ("idn", "idf", -1),
+                          ("mlp", "ml", 1024), ("mln", "ml", -1024), ("e4n", "e4", 1024), ("idz", "idf", ZS), ("mlz", "ml", -1024 * ZS), ("e4z", "e4", 1024 * ZS)):
+        vts(out, in0, float(f))
+    add("v", lambda: v.tensor_tensor(t.bq[:], t.bq1[:], t.bq2[:], ALU.add), [C("bq1"), C("bq2")], [C("bq")], cv(256))
+    add("v", lambda: v.tensor_scalar(t.cz[:], t.ck[:, 0::16], -0.125, 1023 / 8, ALU.mult, ALU.add), [C("ck")], [C("cz")], cv(1))
 
     def tiles(b):
         def L(n, a=0, e=None):
-            w = TILE[n][0]
-            return (n, w * b + a, w * b + (w if e is None else e))
+            return (n, TILE[n] * b + a, TILE[n] * b + (TILE[n] if e is None else e))
 
         def X(n, a=0, e=None, p=128, st=1):
             _, c0, c1 = L(n, a, e)
             return t[n][0:p, c0:c1:st] if st > 1 else t[n][0:p, c0:c1]
-        return L, X, [nm("pb", 2 * b), nm("pb", 2 * b + 1)], nm("pb", 4 + b), nm("pb", 6 + b)
-    ALL = lambda bank: (bank, 0, 512)
+        return L, X
 
-    def slice_block(s, b):
-        L, X, LX, RB, QB = tiles(b)
-        o, q0 = mi(s, b), MW * (NB * s + b)
+    def send(out, in_, R, W, sem, lat):
+        snd = add("g", lambda: g.remote_dma(out, in_, t.sem[sem], t.sem.lsem, npid, nrid, nmask), [R], (), 1.0, "lsem", -nne)
+        add("r", [], (), [W], lat, sem, nne, (snd,))
+
+    def gather(q, out, win, R, W, n):
+        add(q, (lambda: sc.activation(out, win, AF.Copy)) if q == "s" else (lambda: v.tensor_copy(out, win)), R, [W], cg(n))
+
+    def block_step(s, b, st):
+        L, X = tiles(b)
+        RB, QB = BANK[b]
+        o, k0 = MW * (NB * s + b), 8 * (NB * s + b)
         U, UR = t.minb[:, o:o + LB], ("minb", o, o + LB)
         cs, ce = CB * b, CB * b + CB
-        k0 = 8 * (NB * s + b)
-        MI, MIR = t.mia[:, k0:k0 + H], ("mia", k0, k0 + H)
-        add("v", lambda: v.tensor_scalar(X("li", 0, H), MI, 1023, None, ALU.bitwise_and), [MIR], [L("li")], cv(H))
-        add("v", lambda: v.tensor_scalar(X("ls", 0, H), X("li", 0, H), -1.0, 1023.0, ALU.mult, ALU.add), [L("li")], [L("ls")], cv(H))
-        add("v", lambda: v.tensor_copy(X("co"), t.cw[:, cs:ce].indirect(X("ls", 0, H))), [("cw", cs, ce), L("ls")], [L("co")], cg(LB))
-        add("s", lambda: sc.activation(X("cf"), t.cw[:, cs:ce].indirect(X("ls", 0, H)), AF.Copy), [("cw", cs, ce), L("ls")], [L("cf")], cg(LB))
-        add("s", lambda: sc.activation(X("pg_"), t.pw[:, cs:ce].indirect(X("ls", 0, H)), AF.Copy), [("pw", cs, ce), L("ls")], [L("pg_")], cg(LB))
-        add("t", [lambda: te.matmul(t[QB][:, 64:64 + LB], t.idb[:], X("pg_"), True, False), lambda: te.matmul(t[QB][:, 64:64 + LB], t.idb[:], t.r16[:], False, True)],
-            [IDB, L("pg_"), ("r16", 0, LB)], [ALL(QB)], ct(128))
-        add("v", lambda: v.tensor_copy(X("po"), t[QB][:, 64:64 + LB]), [ALL(QB)], [L("po")], cv(LB))
-        for h in range(2):
-            add("t", lambda h=h: te.matmul(t[LX[h]][:], t.limt[:, 128 * s:128 * s + 128], t.ex[:, cs + 512 * h:cs + 512 * h + 512], True, True),
-                [("limt", 128 * s, 128 * s + 128), ("ex", 0, 2048)], [ALL(LX[h])], ct(512))
+        limt, LIM = t.limt[:, 128 * s:128 * s + 128], [("limt", 128 * s, 128 * s + 128), C("ex")]
+        ls, LS, k1 = t.eout[:, k0:k0 + H], ("eout", k0, k0 + 8), k0 + 8 * NB
 
-        def piece(st, u):
-            p0, p1, l0, l1 = CS * u, CS * u + CS, LS * u, LS * u + LS
-            lb, c0, DB = LX[p0 // 512], p0 % 512, (QB, RB)[u % 2]
-            win = lambda: X("f", p0, p1).indirect(X("po", l0, l1))
-            add("s", lambda: sc.activation(X("f", p0, p1), t.xw[:].indirect(X("co", l0, l1)), AF.Copy), [("xw", 0, 4096), L("co", l0, l1)], [L("f", p0, p1)], cg(CS))
-            gio = [L("f", p0, p1), L("po", l0, l1)], [L("gq", p0, p1)], cg(CS)
-            if (st, u) in GS:
-                add("s", lambda: sc.activation(X("gq", p0, p1), win(), AF.Copy), *gio)
+        def places(n):
+            add("v", lambda: v.tensor_scalar(X("li", 0, n * H), X("kc", 15, n * LB, 128, 16), 1023, None, ALU.bitwise_and), [L("kc")], [L("li")], cv(H))
+            add("v", lambda: v.tensor_scalar(t.eout[:, k0:k0 + n * H], X("li", 0, n * H), -1.0, 1023.0, ALU.mult, ALU.add), [L("li")], [LS], cv(H))
+
+        def chosen():
+            add("v", lambda: v.tensor_tensor_scan(X("kc", 0, LB), t.sm[:], U, 0.0, ALU.mult, ALU.max), [C("sm"), UR], [L("kc", 0, LB)], cv(LB))
+
+        def head():
+            if s == 0:
+                cur[:] = [0, -1, {}]
+                chosen()
+                places(1)
+                cur[:] = [b, st, {("v", "kc"): 1}]
+                cwin, pwin, rd = t.pgi[:, cs:ce].indirect(ls), t.pw[:, cs:ce].indirect(ls), (("pgi", cs, ce), ("pw", cs, ce), LS)
             else:
-                add("v", lambda: v.tensor_copy(X("gq", p0, p1), win()), *gio)
-            add("t", [lambda: te.matmul(t[DB][:, 256:256 + CS], t.idb[:], X("f", p0, p1), True, False), lambda: te.matmul(t[DB][:, 256:256 + CS], t.nid[:], X("gq", p0, p1), False, True)],
-                [IDB, NID, L("f", p0, p1), L("gq", p0, p1)], [ALL(DB)], ct(2 * CS))
-            add("s", lambda: sc.activation(X("a", p0, p1), t[DB][:, 256:256 + CS], AF.Abs), [ALL(DB)], [L("a", p0, p1)], cv(CS))
-            add("v", lambda: v.tensor_tensor(X("m", p0, p1), X("a", p0, p1), t[lb][:, c0:c0 + CS], ALU.is_le), [L("a", p0, p1), ALL(lb)], [L("m", p0, p1)], cv(CS))
+                mi = t.mia[:, k0:k0 + H]
+                cwin, pwin, rd = X("cc").indirect(mi), X("pc").indirect(mi), (L("cc"), L("pc"), ("mia", k0, k0 + 8))
+            gather("v", X("co"), cwin, [rd[0], rd[2]], L("co"), LB)
+            gather("s", X("pg_"), pwin, [rd[1], rd[2]], L("pg_"), LB)
+            for (n, f, c0) in (("ax", 5.0, float(1 + OFF + THR)), ("cx", 1.0, float(OFF + THR))):
+                if s == 0:
+                    add("v", lambda n=n, f=f, c0=c0: v.tensor_scalar(X(n), cwin, f, c0, ALU.mult, ALU.add), [rd[0], rd[2]], [L(n)], cg(LB))
+                else:
+                    add("s", lambda n=n, f=f, c0=c0: sc.activation(X(n), cwin, AF.Copy, bias=c0, scale=f), [rd[0], rd[2]], [L(n)], cg(LB))
+            add("s", lambda: sc.activation(X("fq"), X("ax"), AF.Copy, bias=FQ - (2047.5 + OFF + THR) / 4096, scale=1.0 / 4096), [L("ax")], [L("fq")], cv(LB))
+            mm(QB, 64, [(t.idb[:], X("pg_"), LB, False, [C("idb"), L("pg_")]), (t.idb[:], t.r16[:], LB, False, [C("r16")])])
+            add("v", lambda: v.tensor_copy(X("po"), t[QB][:, 64:64 + LB]), [ALL(QB)], [L("po")], cv(LB))
+
+        def others():
+            if s > 0:
+                chosen()
+            add("v", lambda: v.tensor_tensor(X("se"), X("kc", 0, LB).indirect(t.cl[:]), U, ALU.is_equal), [L("kc", 0, LB), C("cl"), UR], [L("se")], cg(LB))
+            if s == N - 1:
+                return places(1)
+            mm(RB, 256, [(t.idf[:], U, LB, True, [C("idf"), UR]), (t.nbig[:], X("se"), LB, False, [C("nbig"), L("se")])])
+            add("v", lambda: v.tensor_tensor_scan(X("kc", LB), t.sm[:], t[RB][:, 256:256 + LB], 0.0, ALU.mult, ALU.max), [C("sm"), ALL(RB)], [L("kc", LB)], cv(LB))
+            places(2)
+            send(t.ein[:, k1:k1 + 2 * H], t.eout[:, k0:k0 + 2 * H], LS, ("ein", k1, k1 + 8), "e%d_%d" % (s + 1, b), HOP)
+            add("v", lambda: v.tensor_tensor(X("lz", 0, H), X("li", 0, H), X("kc", LB + 15, 2 * LB, 128, 16), ALU.subtract), [L("li"), L("kc", LB)], [L("lz")], cv(H))
+
+        def candidates():
+            for (n, WIN) in (("pc", "pw"), ("cc", "cw")):
+                add("s", [lambda d=d, n=n, WIN=WIN: sc.activation(X(n, 1 - d, 2 * LB, 128, 2), t[WIN][:, cs:ce].indirect(t.ein[:, k1 + H * d:k1 + H * d + H]), AF.Copy) for d in range(2)],
+                    [(WIN, cs, ce), ("ein", k1, k1 + 8)], [L(n)], 2 * cg(LB))
+
+        def piece(u):
+            p0, p1, DB = 256 * u, 256 * u + 256, "pb%d" % (2 * NB + u)
+            mm(DB, 256, [(limt, t.ex[:, cs + p0:cs + p1], 256, False, LIM)])
+            mm(DB, 0, [(t.idb[:], X("f", p0, p1), 256, False, [C("idb"), L("f", p0, p1)])], 128, True, False)
+            mm(DB, 0, [(t.nid[:], X("gq", p0, p1), 256, False, [C("nid"), L("gq", p0, p1)])], 128, False, True)
+            add("s", lambda: sc.activation(X("a", p0, p1), t[DB][:, 0:256], AF.Abs, scale=1.0 / WT), [ALL(DB)], [L("a", p0, p1)], cv(256))
+            add("v", lambda: v.tensor_tensor(X("m", p0, p1), X("a", p0, p1), t[DB][:, 256:512], ALU.is_le), [L("a", p0, p1), ALL(DB)], [L("m", p0, p1)], cv(256))
+
+        def count():
+            mm(QB, 224 + 8 * st, [(X("pa"), t.bo[:, 0::16], 8, False, [L("pa"), C("bo")])], LB)
 
         def key_and_hop():
-            add("t", lambda: te.matmul(t[QB][0:LB, 232:240], X("pa"), t.bo[:, 0::16], True, True), [L("pa"), BO], [ALL(QB)], ct(64))
-            add("t", lambda: te.matmul(t[LX[1]][0:LB, 0:128], X("pa"), t.bo[:], True, True), [L("pa"), BO], [ALL(LX[1])], ct(128))
-            add("s", lambda: sc.activation(X("f8", 0, 16, LB), t[QB][0:LB, 224:240], AF.Relu, bias=t.bias[0:LB, 0:1], accum_out=X("mm", 0, 1, LB)),
-                [ALL(QB), ("bias", 0, 1)], [L("f8"), L("mm")], cv(64) + 0.02)
-            add("v", lambda: v.tensor_tensor(X("mk", 0, 128, LB), t.ml[0:LB, :], t[LX[1]][0:LB, 0:128], ALU.mult), [ALL(LX[1]), ML], [L("mk")], cv(128))
-            add("v", lambda: v.tensor_copy(X("mn", 0, 1, LB), X("mm", 0, 1, LB)), [L("mm")], [L("mn")], cv(1))
-            add("v", lambda: v.tensor_scalar(X("od", 0, 1, LB), X("mn", 0, 1, LB), 1, None, ALU.bitwise_and), [L("mn")], [L("od")], cv(1))
-            add("v", lambda: v.tensor_scalar(t.mout[0:LB, q0 + LB:q0 + LB + 1], X("od", 0, 1, LB), t.minb[0:LB, o + LB:o + LB + 1], 1.0, ALU.add, ALU.add),
-                [L("od"), ("minb", o + LB, o + LB + 8)], [("mout", q0 + LB, q0 + LB + 4)], cv(1))
-            add("v", lambda: v.tensor_scalar(X("rb", 0, LB, LB), t.e4s[0:LB, :], t.mout[0:LB, q0 + LB:q0 + LB + 1], None, ALU.mult),
-                [("mout", q0 + LB, q0 + LB + 4), ("e4s", 0, LB)], [L("rb")], cv(LB))
-            add("v", lambda: v.tensor_tensor(X("ns"), MI.indirect(t.cl[:, 0:H]), U, ALU.not_equal), [MIR, ("cl", 0, H), UR], [L("ns")], cg(LB))
-            add("s", lambda: sc.activation(X("se"), X("ns"), AF.Copy, bias=1.0, scale=-1.0), [L("ns")], [L("se")], cv(LB))
-            add("v", lambda: v.tensor_tensor(X("ua"), X("ns"), U, ALU.mult), [L("ns"), UR], [L("ua")], cv(2 * LB))
-            N0, N1, S0, S1 = 384, 384 + H, slice(256, 256 + LB), slice(320, 320 + LB)
+            mk, rb = X("mk", 0, 128, LB), X("rb", 0, LB, LB)
+            count()
+            mm(QB, 256, [(X("pa"), t.bo[:], 128, False, [L("pa"), C("bo")])], LB)
+            add("v", lambda: v.tensor_reduce(X("pr", 0, 1, LB), t[QB][0:LB, 224:240], AxisListType.X, ALU.mult), [ALL(QB)], [L("pr")], cv(16))
+            add("v", lambda: v.tensor_tensor(mk, t.ml[0:LB, :], t[QB][0:LB, 256:384], ALU.mult), [ALL(QB), C("ml")], [L("mk")], cv(128))
+            add("v", lambda: v.tensor_scalar(rb, t.e4[0:LB, :], X("pr", 0, 1, LB), 0.0, ALU.mult, ALU.is_lt), [C("e4"), L("pr")], [L("rb")], cv(LB))
             if s < N - 1:
-                for j in range(H):
-                    add("v", lambda j=j: v.tensor_reduce(X("mo", j, j + 1), X("ua", j, None, 128, H), AxisListType.X, ALU.max), [L("ua")], [L("mo", j, j + 1)], cv(16))
-                add("v", lambda: v.tensor_scalar(X("lk", 0, H), X("li", 0, H), 65536.0, None, ALU.add), [L("li")], [L("lk")], cv(4))
-                add("t", [lambda: te.matmul(t[LX[0]][:, N0:N1], t.idf[:], X("lk", 0, H), True, False),
-                          lambda: te.matmul(t[LX[0]][:, N0:N1], X("mk", 0, 128, LB), t.e4n[0:LB, 0:H], False, False)],
-                    [IDF, L("lk"), L("mk"), ("e4n", 0, LB)], [ALL(LX[0])], ct(320))
-                add("t", lambda: te.matmul(t[LX[0]][:, N0:N1], t.ml[0:LB, :], X("rb", 0, H, LB), False, True), [ML, L("rb")], [ALL(LX[0])], ct(64))
-                add("v", lambda: v.tensor_tensor(t.mxo[:, k0:k0 + H], X("mo", 0, H), t[LX[0]][:, N0:N1], ALU.max), [ALL(LX[0]), L("mo")], [("mxo", k0, k0 + H)], cv(8))
-                k1, ks = k0 + 8 * NB, "k%d_%d" % (s + 1, b)
-                snd = add("g", lambda: g.remote_dma(t.mia[:, k1:k1 + H], t.mxo[:, k0:k0 + H], t.sem[ks], t.sem.lsem, npid, nrid, nmask),
-                          [("mxo", k0, k0 + H)], (), 1.0, "lsem", -nne)
-                add("r", [], (), [("mia", k1, k1 + H)], HOP, ks, nne, (snd,))
-            add("t", [lambda: te.matmul(t[LX[0]][:, S0], t.idf[:], t.ck[:], True, False),
-                      lambda: te.matmul(t[LX[0]][:, S0], X("mk", 0, 128, LB), t.e4n[0:LB, :], False, False)],
-                [IDF, CK, L("mk"), ("e4n", 0, LB)], [ALL(LX[0])], ct(320))
-            add("t", lambda: te.matmul(t[LX[0]][:, S0], t.ml[0:LB, :], X("rb", 0, LB, LB), False, True), [ML, L("rb")], [ALL(LX[0])], ct(64))
-            add("v", lambda: v.tensor_tensor(t[LX[0]][:, S1], X("se"), t[LX[0]][:, S0], ALU.mult), [L("se"), ALL(LX[0])], [ALL(LX[0])], cv(LB))
-            add("v", lambda: v.tensor_tensor(t.mout[:, q0:q0 + LB], t[LX[0]][:, S1], X("ua"), ALU.add), [ALL(LX[0]), L("ua")], [("mout", q0, q0 + LB)], cv(LB))
-            add("t", [lambda: te.matmul(t[LX[1]][0:LB, 128:136], t.idf[0:LB, 0:LB], t.minb[0:LB, o + LB + 8:o + MW], True, False)] +
-                [lambda k=k: te.matmul(t[LX[1]][0:LB, 128:136], t.idb[0:LB, 0:LB], X("f8", 8 * k, 8 * k + 8, LB), False, k == 1) for k in range(2)],
-                [IDF, IDB, ("minb", o + LB + 8, o + MW), L("f8")], [ALL(LX[1])], ct(384))
-            add("s", lambda: sc.activation(t.mout[0:LB, q0 + LB + 8:q0 + MW], t[LX[1]][0:LB, 128:136], AF.Copy), [ALL(LX[1])], [("mout", q0 + LB + 8, q0 + MW)], cv(64))
-            hs, no = "h%d_%d" % (s + 1, b), mi(s + 1, b)
-            snd = add("g", lambda: g.remote_dma(t.minb[:, no:no + MW], t.mout[:, q0:q0 + MW], t.sem[hs], t.sem.lsem, npid, nrid, nmask),
-                      [("mout", q0, q0 + MW)], (), 1.0, "lsem", -nne)
-            add("r", [], (), [("minb", no, no + MW)], HOP + 0.5, hs, nne, (snd,))
+                mm(QB, 384, [(t.idb[:], t.cz[:], H, False, [C("idb"), C("cz")]), (t.oneb[0:1, :], t.cy[0:1, :], H, False, [C("oneb"), C("cy")]),
+                             (t.idz[:], X("lz", 0, H), H, True, [C("idz"), L("lz")]), (mk, t.e4z[0:LB, 0::16], H, False, [L("mk"), C("e4z")])], 128, True, False)
+                mm(QB, 384, [(t.mlz[0:LB, :], X("rb", 0, LB, LB, 16), H, False, [C("mlz"), L("rb")])], 128, False, True)
+                add("v", lambda: v.tensor_scalar(t.mxo[:, k0:k0 + H], t[QB][:, 384:384 + H], MAGIC, MAGIC, ALU.add, ALU.subtract), [ALL(QB)], [("mxo", k0, k0 + 8)], cv(8))
+                send(t.mia[:, k1:k1 + H], t.mxo[:, k0:k0 + H], ("mxo", k0, k0 + 8), ("mia", k1, k1 + 8), "k%d_%d" % (s + 1, b), HOP)
+            add("v", lambda: v.tensor_scalar(X("f8", 0, 16, LB), t[QB][0:LB, 224:240], 2.0, 0.0, ALU.mult, ALU.max), [ALL(QB)], [L("f8")], cv(16))
+            old = [(t.idf[:], t.ck2[:], LB, True, [C("idf"), C("ck2")]), (t.idn[:], U, LB, True, [C("idn"), UR])]
+            new = [(mk, t.e4n[0:LB, :], LB, False, [L("mk"), C("e4n")]), (t.mln[0:LB, :], rb, LB, False, [C("mln"), L("rb")])]
+            grown = [(t.idf[:], U, LB, True, [C("idf"), UR]), (t.mlp[0:LB, :], t.e4[0:LB, :], LB, False, [C("mlp"), C("e4")])]
+            late = [(t.mlp[0:LB, :], rb, LB, False, [C("mlp"), L("rb")]), (t.idf[:], X("w"), LB, True, [C("idf"), L("w")])]
 
-        def step(st):
-            BK = (QB, RB)[st]
-            if st == 1:
-                add("v", lambda: v.tensor_copy(X("cf"), X("ci")), [L("ci")], [L("cf")], cv(LB))
-            for u in range(NS):
-                piece(st, u)
-            add("s", lambda: sc.activation(X("a5"), X("cf"), AF.Copy, bias=float(1 - 17 * KB), scale=5.0), [L("cf")], [L("a5")], cv(LB))
-            add("s", lambda: sc.activation(X("ax"), X("cf"), AF.Copy, bias=float(1 - 17 * KB + THR), scale=5.0), [L("cf")], [L("ax")], cv(LB))
-            add("t", lambda: te.matmul(t[RB][:, 0:LB], t.idf[:], X("a5"), True, False), [IDF, L("a5")], [ALL(RB)], ct(256))
-            add("t", [lambda k=k: te.matmul(t[RB][:, 0:LB], t.es[:, 128 * k:128 * k + 128], X("a", k, None, 128, 16), False, False) for k in range(16)],
-                [("es", 0, 2048), L("a")], [ALL(RB)], ct(1024))
-            add("t", [lambda k=k: te.matmul(t[RB][:, 0:LB], t.ew[:, 128 * k:128 * k + 128], X("m", k, None, 128, 16), False, k == 15) for k in range(16)],
-                [("ew", 0, 2048), L("m")], [ALL(RB)], ct(1024))
+            def change(bank):
+                add("v", lambda: v.tensor_tensor(X("w"), X("se"), t[bank][:, 256:256 + LB], ALU.mult), [L("se"), ALL(bank)], [L("w")], cv(LB))
 
-            def qc():
-                add("t", lambda: te.matmul(t[BK][:, 128:128 + LB], t.idf[:], X("cf"), True, False), [IDF, L("cf")], [ALL(BK)], ct(256))
-
-            def qp():
-                add("t", lambda: te.matmul(t[BK][:, 128:128 + LB], t.bq[:], X("pa"), False, True), [("bq", 0, 128), L("pa")], [ALL(BK)], ct(64))
-
-            def bm():
-                add("v", lambda: v.tensor_tensor(X("bm"), X("ax"), t[RB][:, 0:LB], ALU.min), [L("ax"), ALL(RB)], [L("bm")], cv(LB))
-            if st == 0:
-                qc()
-            add("v", lambda: v.tensor_scalar(X("pa"), t[RB][:, 0:LB], float(THR - 17 * KB), None, ALU.is_ge), [ALL(RB)], [L("pa")], cv(LB))
-            if st == 0:
-                qp()
-                bm()
+            def matches():
+                mm(QB, 128 + LB, [(t.idf[0:LB, :], t.minb[0:LB, o + LB:o + MW], 8, True, [C("idf"), ("minb", o + LB, o + MW)])] +
+                   [(t.idb[0:LB, :], X("f8", 8 * k, 8 * k + 8, LB), 8, False, [C("idb"), L("f8")]) for k in range(2)])
+            hs = "h%d_%d" % (s + 1, b)
+            if s < N - 1:
+                mm(QB, 256, old[:1], 128, True, False)
+                mm(QB, 256, old[1:] + new, 128, False, True)
+                change(QB)
+                matches()
+                mm(QB, 128, grown + late)
+                no = o + MW * NB
+                add("s", lambda: sc.activation(t.mout[:, o:o + MW], t[QB][:, 128:128 + MW], AF.Copy), [ALL(QB)], [("mout", o, o + MW)], cv(MW))
+                send(t.minb[:, no:no + MW], t.mout[:, o:o + MW], ("mout", o, o + MW), ("minb", no, no + MW), hs, HOP + 0.5)
             else:
-                key_and_hop()
-                bm()
-                qc()
-                qp()
-            add("v", lambda: v.tensor_tensor(X("yi"), X("bm"), t[BK][:, 128:128 + LB], ALU.min), [L("bm"), ALL(BK)], [L("yi")], cv(LB))
+                mm(RB, 256, old, 128, True, False)
+                matches()
+                mm(QB, 128, grown + [(t.idn[:], t.ck[:], LB, True, [C("idn"), C("ck")])], 128, True, False)
+                mm(RB, 256, new, 128, False, True)
+                change(RB)
+                mm(QB, 128, late, 128, False, True)
+                f0 = MW * b
+                add("s", [lambda: sc.activation(t.fout[:, f0 + LB:f0 + MW], t[QB][:, 128 + LB:128 + MW], AF.Copy)] +
+                    [lambda j=j: sc.activation(t.fout[:, f0 + j:f0 + LB:H], t[QB][:, 128 + 16 * j:144 + 16 * j], AF.Copy, scale=1.0 / 1024) for j in range(H)],
+                    [ALL(QB)], [("fout", f0, f0 + MW)], (H + 1) * cv(16))
+                send(t.fin[:, f0:f0 + MW], t.fout[:, f0:f0 + MW], ("fout", f0, f0 + MW), ("fin", f0, f0 + MW), hs, HOP + 0.5)
+
+        def passed():
+            add("v", lambda: v.tensor_scalar(X("pa"), t[RB][:, 0:LB], float(THR + OFF), 31.0 / 32, ALU.is_ge, ALU.subtract), [ALL(RB)], [L("pa")], cv(LB))
+
+        def low():
             add("v", lambda: v.tensor_scalar(X("ci"), X("yi"), 4095, None, ALU.bitwise_and), [L("yi")], [L("ci")], cv(LB))
-            if st == 0:
-                add("v", lambda: v.tensor_copy(X("co"), X("ci")), [L("ci")], [L("co")], cv(LB))
-                add("t", lambda: te.matmul(t[QB][0:LB, 224:232], X("pa"), t.bo[:, 0::16], True, True), [L("pa"), BO], [ALL(QB)], ct(64))
+        if st == 0:
+            head()
+        for n in ("f", "gq"):
+            l0 = 0
+            for (k, q) in ((CUTS[b][st], "s"), (32 - CUTS[b][st], "v")) * 2:
+                win, WIN, off = (t.xw[:, 0:4096 << st], ("xw", 0, 4096 << st), "co") if n == "f" else (X("f", 0, 16 * (l0 + k)), L("f", 0, 16 * (l0 + k)), "po")
+                gather(q, X(n, 16 * l0, 16 * (l0 + k)), win.indirect(X(off, l0, l0 + k)), [WIN, L(off, l0, l0 + k)], L(n, 16 * l0, 16 * (l0 + k)), 16 * k)
+                l0 += k
+        for u in range(H):
+            piece(u)
+        if st == 1:
+            add("s", lambda: sc.activation(X("ax"), X("cf"), AF.Copy, bias=float(1 + OFF + THR), scale=5.0), [L("cf")], [L("ax")], cv(LB))
+        mm(RB, 0, [(t.idf[:], X("ax"), LB, True, [C("idf"), L("ax")]), (t.thb[0:1, :], t.oneb[0:1, 0:LB], LB, False, [C("thb"), C("oneb")])], 128, True, False)
+        for n in "am":
+            mm(RB, 0, [(t.es[:, 128 * k:128 * k + 128], X(n, k, CB, 128, 16), LB, False, [C("es"), L(n)]) for k in range(16)], 128, False, n == "m")
+        if st == 0:
+            mm(QB, 128, [(t.idf[:], X("ax"), LB, True, [C("idf"), L("ax")]), (t.n4k[:], X("fq"), LB, False, [C("n4k"), L("fq")])], 128, True, False)
+            passed()
+            add("v", lambda: v.tensor_tensor(X("yi"), X("cx"), t[RB][:, 0:LB], ALU.min), [L("cx"), ALL(RB)], [L("yi")], cv(LB))
+            low()
+            mm(QB, 128, [(t.bk[:], X("pa"), LB, False, [C("bk"), L("pa")])], 128, False, True)
+            add("v", lambda: v.tensor_tensor(X("cf"), X("ci"), t[QB][:, 128:128 + LB], ALU.max), [L("ci"), ALL(QB)], [L("cf")], cv(LB))
+            add("v", lambda: v.tensor_copy(X("co"), X("cf")), [L("cf")], [L("co")], cv(LB))
+            count()
+            others()
+        else:
+            passed()
+            add("v", lambda: v.tensor_tensor(X("bm"), X("ax"), t[RB][:, 0:LB], ALU.min), [L("ax"), ALL(RB)], [L("bm")], cv(LB))
+            key_and_hop()
+            mm(RB, 128, [(t.idf[:], X("cf"), LB, True, [C("idf"), L("cf")]), (t.bq[:], X("pa"), LB, False, [C("bq"), L("pa")])])
+            add("v", lambda: v.tensor_tensor(X("yi"), X("bm"), t[RB][:, 128:128 + LB], ALU.min), [L("bm"), ALL(RB)], [L("yi")], cv(LB))
+            low()
+            add("v", lambda: v.tensor_copy(t.cw[:, cs:ce].indirect(ls), X("ci")), [L("ci"), LS], [("cw", cs, ce)], 0.05 + 3.8 * LB * CYC)
+            if s < N - 1:
+                candidates()
             else:
-                add("v", lambda: v.tensor_copy(t.cw[:, cs:ce].indirect(X("ls", 0, H)), X("ci")), [L("ci"), L("ls")], [("cw", cs, ce)], (0.05 + 3.8 * LB * CYC) * FAC)
-        step(0)
-        step(1)
-        if s == N - 1:
-            add("y", lambda: g.sync.dma_start(t.yg[:, cs:ce], t.cw[:, cs:ce]), [("cw", cs, ce)], (), 0.06, nm("oyg", b), 16, (), 4.0)
+                add("y", lambda: g.sync.dma_start(t.yg[:, cs:ce], t.cw[:, cs:ce]), [("cw", cs, ce)], (), 0.06, nm("oyg", b), 16, (), 4.0)
 
     for s in range(N):
-        for b in range(NB):
-            cur[0] = BON * b
-            slice_block(s, b)
-    cur[0] = 0.0
+        for st in range(2):
+            for b in range(NB):
+                cur[:] = [NB * s + b, st, {}]
+                block_step(s, b, st)
+    cur[:] = [NB * N + 2, -1, {}]
 
     def home(b):
-        L, X, LX, RB, QB = tiles(b)
-        o = mi(N, b)
-        L0, L1 = t[LX[0]][0:LB, 256:384], t[LX[1]][0:8, 0:LB]
-        add("s", lambda: sc.activation(X("rb", 0, LB, LB), t.e4[0:LB, :], AF.Identity, scale=t.minb[0:LB, o + LB:o + LB + 1]), [E4, ("minb", o + LB, o + LB + 8)], [L("rb")], cv(LB))
-        add("t", [lambda: te.matmul(L0, t.minb[:, o:o + LB], t.idp[:], True, False), lambda: te.matmul(L0, t.ck[:], t.idn[:], False, False),
-                  lambda: te.matmul(L0, X("rb", 0, LB, LB), t.ml[0:LB, :], False, True)],
-            [("minb", o, o + LB), ("idn", 0, 128), CK, ("idp", 0, 128), L("rb"), ML], [ALL(LX[0])], ct(1152))
-        add("v", lambda: v.tensor_copy(X("vo", 0, 128, LB), L0), [ALL(LX[0])], [L("vo")], cv(128))
+        L, X = tiles(b)
+        RB, QB = BANK[b]
+        f0 = MW * b
+        FR = ("fin", f0, f0 + MW)
+        mm(QB, 256, [(t.fin[:, f0:f0 + LB], t.idb[:], 128, False, [FR, C("idb")])], LB)
+        mm(RB, 0, [(t.fin[0:LB, f0 + LB:f0 + MW], t.idb[0:LB, 0:LB], LB, False, [FR, C("idb")])], 8)
+        add("v", lambda: v.tensor_copy(X("vo", 0, 128, LB), t[QB][0:LB, 256:384]), [ALL(QB)], [L("vo")], cv(128))
+        add("s", lambda: sc.activation(X("yo", 0, LB, 8), t[RB][0:8, 0:LB], AF.Copy), [ALL(RB)], [L("yo")], cv(64))
         for (q, k0) in (("y", 0), ("s", 4)):
             add(q, [lambda k=k, q=q: eng[q].dma_start(t.yv[16 * k:16 * k + 16, LB * b:LB * b + LB], X("vo", 16 * k, 16 * k + 16, LB)) for k in range(k0, k0 + 4)],
                 [L("vo")], (), 0.24, nm("oyv", b), 64 if q == "y" else 128, (), 2.0)
-        add("t", lambda: te.matmul(L1, t.minb[0:LB, o + LB + 8:o + MW], t.idf[0:LB, 0:LB], True, True), [("minb", o + LB + 8, o + MW), IDF], [ALL(LX[1])], ct(256))
-        add("s", lambda: sc.activation(X("yo", 0, LB, 8), L1, AF.Copy), [ALL(LX[1])], [L("yo")], cv(64))
         add("y", lambda: g.sync.dma_start(t.ym[:, LB * b:LB * b + LB], X("yo", 0, LB, 8)), [L("yo")], (), 0.06, nm("oym", b), 16, (), 2.0)
     for b in range(NB):
         home(b)
@@ -419,15 +449,15 @@ def rank_program(g, core, T, topo):
             eng[q].wait_ge(t.sem[sem], val)
             for (a, w) in list(jk.items()) + [(sem, val)]:
                 kn[a] = max(kn.get(a, 0), w)
-        ins = None
         for f in d["f"]:
             ins = f()
             if d["sem"] and d["val"] > 0:
                 ins.then_inc(t.sem[d["sem"]], 16)
+            if d["sem"] is None and (q != "t" or f is d["f"][-1]):
+                cnt[csem[q]] = cnt.get(csem[q], 0) + 1
+                ins.then_inc(t.sem[csem[q]], 1)
         if d["sem"] is None:
             sem = csem[q]
-            cnt[sem] = cnt.get(sem, 0) + 1
-            ins.then_inc(t.sem[sem], 1)
             tok[i] = (sem, cnt[sem], dict(kn))
             total[sem] = cnt[sem]
         elif d["val"] > 0:

from concourse.bass import DstId, RemoteDMATransfer
from concourse.mybir import AluOpType as ALU, AxisListType, ActivationFunctionType as AF

N, NB = 8, 2
LB = 128 // NB
H, CB, MW = LB // 16, 16 * LB, LB + 8
CUTS = ((16, 18), (20, 20))
FIRST, PERIOD = 10.0, 16.365
TABLE = {
    (0, 0, "v"): "co1@0.00 f1@0.37 po1@0.83 f2@0.88 gq1@1.27 gq2@1.66 m1@2.63 m2@2.84 m3@3.07 m4@3.49 kc1@3.71 yi1@4.59 pa1@4.64 se1@4.69 ci1@4.87 cf1@5.23 co2@5.52 kc2@7.44 li1@7.83 eout1@8.28 lz1@8.58",
    (0, 0, "s"): "pg_1@0.17 ax1@0.31 f1@0.45 f2@0.83 gq1@1.22 gq2@1.67 a1@2.18 a2@2.39 a3@2.62 a4@2.84 fq1@3.05 cx1@3.10",
    (0, 0, "t"): "P71@-1.84 P61@-1.74 P51@-1.63 P41@-1.40 Q1@0.54 R1@1.00 P52@1.13 P42@1.23 P62@1.45 P72@1.56 P43@1.84 P53@1.94 P63@2.29 P73@2.39 Q2@3.34 R2@3.47 R3@3.94 Q3@4.93 R4@5.07 Q4@5.68",
    (0, 0, "g"): "eout1@8.57",
    (0, 1, "v"): "f1@5.88 f2@6.65 gq1@7.49 gq2@7.94 m1@8.93 m2@9.19 m3@9.48 m4@9.71 pa1@10.80 bm1@11.21 pr1@11.40 mk1@11.46 rb1@11.69 mxo1@12.24 f81@12.29 w1@13.28 yi1@13.34 ci1@13.62 cw1@14.21",
    (0, 1, "s"): "f1@6.13 f2@6.99 gq1@7.42 gq2@8.03 a1@8.48 ax1@8.69 a2@8.75 a3@9.03 a4@9.27 pc1@12.83 mout1@14.57 fout1@14.57 cc1@14.70",
    (0, 1, "t"): "P41@6.67 P51@6.88 P42@6.98 P52@7.09 P61@7.63 P43@8.14 P53@8.25 P71@8.48 P62@8.58 P63@8.70 P72@8.83 P73@8.93 R1@9.03 R2@9.74 R3@10.16 Q1@11.09 Q2@11.12 Q3@11.80 Q4@11.98 R4@12.11 Q5@12.58 Q6@12.69 Q7@13.93 Q8@14.08",
    (0, 1, "g"): "mxo1@12.53 mout1@14.87 fout1@14.87",
    (1, 0, "v"): "co1@3.36 f1@3.76 po1@4.16 f2@4.21 gq1@4.93 gq2@5.57 m1@6.22 m2@6.43 m3@7.01 m4@7.22 kc1@7.89 se1@8.34 pa1@8.48 yi1@8.53 ci1@8.82 cf1@9.14 co2@9.43 kc2@9.93 li1@10.59 eout1@11.16 lz1@11.27",
    (1, 0, "s"): "ax1@3.36 pg_1@3.49 f1@3.73 f2@4.20 gq1@4.67 gq2@5.14 a1@5.71 a2@5.92 a3@6.56 a4@6.78 cx1@7.84 fq1@7.98",
    (1, 0, "t"): "Q1@3.88 P41@4.35 P61@4.45 P71@4.56 P51@4.66 P42@4.76 P52@4.95 P43@5.37 P53@5.47 P72@5.58 P62@5.71 P63@5.84 P73@6.11 R1@6.21 R2@7.22 R3@7.73 Q2@8.35 Q3@8.80 R4@9.16 Q4@9.48",
    (1, 0, "g"): "eout1@11.45",
    (1, 1, "v"): "f1@9.98 f2@10.28 gq1@10.86 gq2@11.75 m1@12.35 m2@12.56 m3@12.79 m4@13.07 pa1@14.16 bm1@14.47 pr1@14.76 mk1@14.81 rb1@15.05 yi1@15.20 ci1@15.48 mxo1@15.60 f81@15.65 cw1@15.77 w1@16.50",
    (1, 1, "s"): "ax1@9.48 f1@9.72 f2@10.19 gq1@10.66 gq2@11.13 a1@11.71 a2@11.92 a3@12.34 a4@12.62 pc1@15.28 cc1@16.26 fout1@17 mout1@17.97",
    (1, 1, "t"): "P41@9.38 P51@9.64 P52@10.57 P71@10.67 R1@10.77 P61@10.90 P72@11.17 P42@11.27 P43@11.37 P53@11.48 P62@11.58 P63@12.01 P73@12.28 R2@13.07 R3@13.52 Q1@14.45 Q2@14.48 R4@14.83 Q3@15.16 Q4@15.34 Q5@15.94 Q6@16.04 Q7@16.96 Q8@17.11",
    (1, 1, "g"): "mxo1@15.89 fout1@17.3 mout1@18.27",
}
START = {(0, 0, "s"): "pg_1@.8", (0, 0, "v"): "ax1@.15 cx1@.2", (1, 0, "v"): "ax1@4.3 po1@4.75 cx1@5.3", (1, 0, "s"): "pg_1@4.1",
         (0, -1, "v"): "xw1@.5 xw2@.6 xw3@.7 xw4@2.05 cw5@13.4 cw6@13.7 cw7@14.3 cw8@14.6", (0, 0, "t"): "Q1@1.3"}
END = {(0, 1, "t"): "R4@11.3 R5@12 R6@14.55 Q5@14.1", (0, 1, "v"): "yi1@14.95 ci1@15.3 cw1@15.7", (1, 1, "t"): "R4@14.6 Q3@14.9 Q4@15 R5@15.3 Q5@15.9 R6@16", (1, 1, "v"): "f81@14.9 w1@15.6 yi1@16.3 ci1@16.6 cw1@16.9"}
KB = 1 << 20
WT = 1 << 16
THR = 10 * WT
OFF = -33 * KB // 32
FQ = 151
KF = 2 * (4096 * (FQ + 1) - OFF - THR)
NEW = 15872 - 1024
BIG = 65536.0
ZS = 1.0 / (1 << 17)
MAGIC = 1.5 * (1 << 23)

SCRATCH = {"xw": ("sbuf", [128, 8192], "bfloat16"), "pw": ("sbuf", [128, 2048], "bfloat16"), "pgi": ("sbuf", [128, 2048], "int32"),
           "cw": ("sbuf", [128, 2048], "float32"), "es": ("sbuf", [128, 2048], "bfloat16"), "ex": ("sbuf", [128, 2048], "bfloat16"),
           "limt": ("sbuf", [128, 128 * N], "bfloat16"), "minb": ("sbuf", [128, MW * NB * N], "float32"), "mout": ("sbuf", [128, MW * NB * N], "float32"),
           "fin": ("sbuf", [128, MW * NB], "bfloat16"), "fout": ("sbuf", [128, MW * NB], "bfloat16")}
for _w, _d, _names in ((8 * NB * N, "uint16", "mia mxo ein eout"), (128, "int32", "vt ix ix2"), (128, "float32", "onef idf idn idz bq1 bq2"),
                       (128, "bfloat16", "vtb limo oneb posb thb idb nid nbig n4k bo0 bo bq bk pmt ml mlp mln mlz"), (LB, "int32", "ka ka2 kb"),
                       (LB, "float32", "ck ck2 sm"), (LB, "bfloat16", "r16 e4a e4 e4n e4z"), (H, "int32", "cli"), (H, "uint16", "cl"), (H, "bfloat16", "cz cy")):
    for _n in _names.split():
        SCRATCH[_n] = ("sbuf", [128, _w], _d)
TILE = {}
for _w, _d, _names in ((CB, "bfloat16", "f gq a m"), (2 * LB, "float32", "cc vo"), (2 * LB, "bfloat16", "pc mk"), (2 * LB, "int32", "kc"), (LB, "uint16", "co po"),
                       (LB, "float32", "cf ax cx bm w yo"), (LB, "bfloat16", "pg_ fq pa rb se"), (LB, "int32", "yi ci"), (16, "bfloat16", "f8"), (8, "int32", "li"), (4, "float32", "lz pr")):
    for _n in _names.split():
        TILE[_n] = _w
        SCRATCH[_n] = ("sbuf", [128, NB * _w], _d)
for _b in range(8):
    SCRATCH["pb%d" % _b] = ("psum", [128, 512], "float32")

SEMAPHORES = ["qv", "qs", "qt", "qg", "lsem", "limr", "dlim", "dvvy", "dvvs", "dxt"]
SEMAPHORES += ["%s%d" % (n, b) for n in ("dpg", "dpre", "oyg", "oyv", "oym") for b in range(NB)]
SEMAPHORES += ["h%d_%d" % (s, b) for s in range(1, N + 1) for b in range(NB)] + ["%s%d_%d" % (n, s, b) for n in "ke" for s in range(1, N) for b in range(NB)]

CYC, WAKE, XG, PEC, HOP = 0.00083, 0.2, 1.56, 0.0004, 4.0


def cv(n):
    return max(64, n) * CYC


def cg(n):
    return 0.055 + XG * n * CYC


def schedule(nodes):
    n = len(nodes)
    pred = [[(j, nodes[j]["lat"] + WAKE if need else WAKE * (nodes[j]["q"] == "r")) for j, need in d["dep"].items()] for d in nodes]
    path, key, busy = [d["c"] + d["lat"] for d in nodes], [0.0] * n, {}
    for i in range(n - 1, -1, -1):
        for j, w in pred[i]:
            path[j] = max(path[j], nodes[j]["c"] + w + path[i])
    read = lambda table: {k + (w.split("@")[0],): float(w.split("@")[1]) for k in table for w in table[k].split()}
    table, ends = read(TABLE), {0: read(START), N - 1: read(END)}
    for i in sorted(range(n), key=lambda i: -path[i]):
        d = nodes[i]
        s, name = d["turn"] // NB, (d["turn"] % NB, d["step"], d["q"], d["name"])
        if d["step"] >= 0 or name in ends[0]:
            key[i] = FIRST + PERIOD * s + ends.get(s, {}).get(name, table.get(name, 0.0))
        elif s > 0:
            key[i] = FIRST + PERIOD * s
        else:
            t, line = max([0.0] + [key[j] + nodes[j]["c"] + w for j, w in pred[i]]), busy.setdefault(d["q"] if d["q"] != "r" else i, [])
            for (a, e) in sorted(line):
                if a < t + d["c"] and t < e:
                    t = e
            line.append((t, t + d["c"]))
            key[i] = t
    for i in range(n):
        key[i] = max([key[i]] + [key[j] + 1e-7 for j, w in pred[i]])
    return sorted(range(n), key=lambda i: key[i])


def rank_program(g, core, T, topo):
    rank = T.rank_of(core)
    if rank is None:
        return
    eng = {"v": g.vector, "s": g.scalar, "t": g.tensor, "g": g, "y": g.sync}
    csem = {"v": "qv", "s": "qs", "t": "qt", "g": "qg"}
    nodes, last, cur = [], {}, [0, -1, {}]
    ROLE = {"pb%d" % k: "RQ"[k % 2] if k < 2 * NB else "P%d" % k for k in range(8)}
    STREAM = ("co", "po", "cw", "f", "kc", "cc", "pc", "eout")

    def add(q, fns, R=(), W=(), c=0.08, sem=None, val=None, after=(), lat=0.0):
        i = len(nodes)
        dep = {}
        for (acc, wr) in ((R, False), (W, True)):
            for (buf, a, b) in acc:
                bank = buf[:2] == "pb"
                rec = last.setdefault(buf, [])
                for (j, ja, jb, jw) in rec:
                    if j == i or (not bank and (ja >= b or jb <= a)):
                        continue
                    same = nodes[j]["q"] == q
                    if not (wr or jw) and (same or not bank):
                        continue
                    need = not (same and (q == "t" or not (jw or buf in STREAM)))
                    dep[j] = dep.get(j, False) or need
                if wr:
                    if bank and q == "t":
                        rec[:] = [r for r in rec if r[0] == i]
                    elif not bank:
                        rec[:] = [r for r in rec if r[0] == i or not (r[1] >= a and r[2] <= b)]
                rec.append((i, a, b, wr))
        for j in after:
            dep[j] = dep.get(j, False)
        name = (list(W) + list(R))[0][0]
        name = ROLE.get(name, name)
        seen = cur[2][q, name] = cur[2].get((q, name), 0) + 1
        nodes.append({"q": q, "f": fns if isinstance(fns, list) else [fns], "dep": dep, "c": c, "sem": sem, "val": val, "lat": lat,
                      "turn": cur[0], "step": cur[1], "name": name + str(seen)})
        return i

    t = T
    nm = lambda n, b: "%s%d" % (n, b)
    v, sc, te = g.vector, g.scalar, g.tensor
    C = lambda n: (n, 0, SCRATCH[n][1][1])
    ALL = lambda bank: (bank, 0, 512)
    BANK = [("pb%d" % (2 * b), "pb%d" % (2 * b + 1)) for b in range(NB)]

    def mm(bank, c0, terms, p=128, start=True, stop=True):
        fns, R, c = [], [], 0.0
        for k, (l, r, n, f32, rd) in enumerate(terms):
            fns.append(lambda l=l, r=r, n=n, k=k: te.matmul(t[bank][0:p, c0:c0 + n], l, r, start and k == 0, stop and k == len(terms) - 1))
            R += rd
            c += max(min(64, p), n) * (4 if f32 else 1) * PEC
        return add("t", fns, R, [ALL(bank)], c)

    prev = {"y": (), "s": ()}

    def load(fns, W, sem, cost, q="y"):
        prev[q] = (add(q, fns, (), W, 0.06 * len(fns), sem, 16 * len(fns), prev[q], cost),)
    for (q, k0) in (("y", 0), ("s", 4)):
        load([lambda k=k, q=q: eng[q].dma_start(t.vt[:, 16 * k:16 * k + 16], t.vv[16 * k:16 * k + 16, :]) for k in range(k0, k0 + 4)], [("vt", 16 * k0, 16 * k0 + 64)], "dvv" + q, 2.5, q)
    load([lambda: g.scalar.dma_start(t.limo[:], t.lim[:])], [C("limo")], "dlim", 2.5, "s")
    for b in range(NB):
        cs, ce = CB * b, CB * b + CB
        load([lambda cs=cs, ce=ce: g.sync.dma_start(t.pgi[:, cs:ce], t.pg[:, cs:ce])], [("pgi", cs, ce)], nm("dpg", b), 4.6 + 8.8 * b)
        if b == 0:
            load([lambda: g.sync.dma_start(t.xw[:, 0:4096], t.xt[:])], [("xw", 0, 4096)], "dxt", 9.6)
        load([lambda cs=cs, ce=ce: g.sync.dma_start(t.pw[:, cs:ce], t.pre[:, cs:ce])], [("pw", cs, ce)], nm("dpre", b), 10.8 + 3.9 * b)

    def vmem(buf, a, b, val):
        add("v", lambda: v.memset(t[buf][:, a:b], val), (), [(buf, a, b)], cv((b - a) * (0.5 if SCRATCH[buf][2] == "bfloat16" else 1)))

    def vts(out, in0, s1, op=ALU.mult):
        add("v", lambda: v.tensor_scalar(t[out][:], t[in0][:], s1, None, op), [C(in0)], [C(out)], cv(C(out)[2]))

    def gen(out, fn, in_=None):
        add("g", fn, [C(in_)] if in_ else (), [C(out)], 0.17 + 2 * C(out)[2] * CYC)
    for (buf, val) in (("onef", 1.0), ("oneb", 1.0), ("posb", 1024.0), ("thb", float(-THR)), ("es", 0.0), ("sm", 1.0), ("cy", 0.5 + NEW * ZS)):
        vmem(buf, 0, C(buf)[2], val)
    add("v", lambda: v.memset(t.sm[:, 0::16], 0.0), (), [C("sm")], cv(1))
    gen("idf", lambda: g.affine_select(t.idf[:], t.onef[:], [[-1, 128]], ALU.is_equal, 0.0, 0, 1), "onef")
    gen("pmt", lambda: g.affine_select(t.pmt[:], t.posb[:], [[-1, 8], [-8, 16]], ALU.is_equal, 0.0, 0, 1), "posb")
    gen("ka", lambda: g.iota(t.ka[:], [[0, LB]], 0, 16))
    gen("kb", lambda: g.iota(t.kb[:], [[-256, H], [-1, 16]], 1023, 0))
    gen("cli", lambda: g.iota(t.cli[:], [[16, H]], 15, 0))
    gen("r16", lambda: g.iota(t.r16[:], [[16, LB]], 0, 0, allow_small_or_imprecise_dtypes=True))
    gen("bo0", lambda: g.affine_select(t.bo0[:], t.oneb[:], [[-16, 8], [0, 16]], ALU.is_ge, 0.0, 0, 1), "oneb")
    gen("bo", lambda: g.affine_select(t.bo[:], t.bo0[:], [[16, 8], [0, 16]], ALU.is_ge, 0.0, 15, -1), "bo0")
    gen("ix", lambda: g.iota(t.ix[:], [[-1, 128]], 128, 1))
    gen("e4a", lambda: g.affine_select(t.e4a[:], t.oneb[:, 0:LB], [[-16, H], [0, 16]], ALU.is_ge, 0.0, 0, 1), "oneb")
    gen("e4", lambda: g.affine_select(t.e4[:], t.e4a[:], [[16, H], [0, 16]], ALU.is_ge, 0.0, 15, -1), "e4a")
    add("v", lambda: v.tensor_copy(t.idb[:], t.idf[:]), [C("idf")], [C("idb")], cv(128))
    add("v", lambda: v.tensor_copy(t.vtb[:], t.vt[:]), [C("vt")], [C("vtb")], cv(128))
    vts("ka2", "ka", 255, ALU.bitwise_and)
    add("v", lambda: v.tensor_tensor(t.ck[:], t.kb[:], t.ka2[:], ALU.subtract), [C("ka2"), C("kb")], [C("ck")], cv(2 * LB))
    vts("ck2", "ck", float(NEW), ALU.add)
    add("v", lambda: v.tensor_copy(t.cl[:], t.cli[:]), [C("cli")], [C("cl")], cv(1))
    for k in range(0, 2048, 256):
        add("v", lambda k=k: v.tensor_copy(t.cw[:, k:k + 256], t.pgi[:, k:k + 256]), [("pgi", k, k + 256)], [("cw", k, k + 256)], cv(256))
    for b in range(NB):
        o, QB = MW * b, BANK[b][1]
        mm(QB, 448, [(t.vtb[:], t.pmt[:, LB * b:LB * b + LB], LB, False, [C("vtb"), C("pmt")])])
        add("v", lambda o=o, QB=QB: v.tensor_tensor(t.minb[:, o:o + LB], t.ck[:], t[QB][:, 448:448 + LB], ALU.add), [ALL(QB), C("ck")], [("minb", o, o + LB)], cv(LB))
        vmem("minb", o + LB, o + MW, 0.0)
    mm("pb0", 0, [(t.limo[:], t.idb[:], 128, False, [C("limo"), C("idb")])])
    add("s", lambda: sc.activation(t.limt[:, 0:128], t.pb0[:, 0:128], AF.Copy), [ALL("pb0")], [("limt", 0, 128)], cv(128))
    nxt = T.cores[(rank + 1) % N]
    nrid, npid, _ = topo.addr(nxt)
    nmask = topo.mask(core, nxt)
    nne = bin(nmask).count("1")
    dst, dsts, mask = [], [], nmask
    for s in range(1, N):
        d = T.cores[(rank + s) % N]
        rid, pid, _ = topo.addr(d)
        mask &= topo.mask(core, d)
        dst.append(DstId(rid=rid, pnc=pid))
        dsts.append(t.limt[:, 128 * s:128 * s + 128])
    ne = bin(mask).count("1")
    limsend = add("g", lambda: g.remote_dma_fused([RemoteDMATransfer(dst_ids=dst, dma_engine_mask=mask, remote_sem=t.sem.limr,
                  srcs=[t.limt[:, 0:128]], dsts=dsts)], local_sem=t.sem.lsem), [("limt", 0, 128)], (), 2.0, "lsem", -ne)
    add("r", [], (), [("limt", 128, 128 * N)], 4.0, "limr", (N - 1) * ne, (limsend,))

    add("s", [lambda k=k: sc.activation(t.ex[:, k::16], t.idb[:], AF.Copy, scale=1.0 / WT) for k in range(16)], [C("idb")], [C("ex")], 16 * cv(128))
    for k in range(16):
        add("v", lambda k=k: v.tensor_scalar(t.es[:, 128 * k + k:128 * k + 128:16], t.bo[:, k::16], float(WT), None, ALU.mult), [C("bo")], [("es", 128 * k, 128 * k + 128)], cv(8))
    for k in range(0, 4096, 1024):
        add("v", lambda k=k: v.tensor_copy(t.xw[:, 4096 + k:5120 + k], t.xw[:, k:k + 1024]), [("xw", k, k + 1024)], [("xw", 4096 + k, 5120 + k)], cv(512))
    vts("ix2", "ix", 15, ALU.bitwise_and)
    vts("ml", "ix2", 0.0, ALU.is_equal)
    for (out, in0, f) in (("bk", "bo", KF), ("n4k", "idb", -4096), ("bq1", "idb", -17 * KB), ("bq2", "bo", KB), ("nid", "idb", -1), ("nbig", "idb", -BIG), ("idn", "idf", -1),
                          ("mlp", "ml", 1024), ("mln", "ml", -1024), ("e4n", "e4", 1024), ("idz", "idf", ZS), ("mlz", "ml", -1024 * ZS), ("e4z", "e4", 1024 * ZS)):
        vts(out, in0, float(f))
    add("v", lambda: v.tensor_tensor(t.bq[:], t.bq1[:], t.bq2[:], ALU.add), [C("bq1"), C("bq2")], [C("bq")], cv(256))
    add("v", lambda: v.tensor_scalar(t.cz[:], t.ck[:, 0::16], -0.125, 1023 / 8, ALU.mult, ALU.add), [C("ck")], [C("cz")], cv(1))

    def tiles(b):
        def L(n, a=0, e=None):
            return (n, TILE[n] * b + a, TILE[n] * b + (TILE[n] if e is None else e))

        def X(n, a=0, e=None, p=128, st=1):
            _, c0, c1 = L(n, a, e)
            return t[n][0:p, c0:c1:st] if st > 1 else t[n][0:p, c0:c1]
        return L, X

    def send(out, in_, R, W, sem, lat):
        snd = add("g", lambda: g.remote_dma(out, in_, t.sem[sem], t.sem.lsem, npid, nrid, nmask), [R], (), 1.0, "lsem", -nne)
        add("r", [], (), [W], lat, sem, nne, (snd,))

    def gather(q, out, win, R, W, n):
        add(q, (lambda: sc.activation(out, win, AF.Copy)) if q == "s" else (lambda: v.tensor_copy(out, win)), R, [W], cg(n))

    def block_step(s, b, st):
        L, X = tiles(b)
        RB, QB = BANK[b]
        o, k0 = MW * (NB * s + b), 8 * (NB * s + b)
        U, UR = t.minb[:, o:o + LB], ("minb", o, o + LB)
        cs, ce = CB * b, CB * b + CB
        limt, LIM = t.limt[:, 128 * s:128 * s + 128], [("limt", 128 * s, 128 * s + 128), C("ex")]
        ls, LS, k1 = t.eout[:, k0:k0 + H], ("eout", k0, k0 + 8), k0 + 8 * NB

        def places(n):
            add("v", lambda: v.tensor_scalar(X("li", 0, n * H), X("kc", 15, n * LB, 128, 16), 1023, None, ALU.bitwise_and), [L("kc")], [L("li")], cv(H))
            add("v", lambda: v.tensor_scalar(t.eout[:, k0:k0 + n * H], X("li", 0, n * H), -1.0, 1023.0, ALU.mult, ALU.add), [L("li")], [LS], cv(H))

        def chosen():
            add("v", lambda: v.tensor_tensor_scan(X("kc", 0, LB), t.sm[:], U, 0.0, ALU.mult, ALU.max), [C("sm"), UR], [L("kc", 0, LB)], cv(LB))

        def head():
            if s == 0:
                cur[:] = [0, -1, {}]
                chosen()
                places(1)
                cur[:] = [b, st, {("v", "kc"): 1}]
                cwin, pwin, rd = t.pgi[:, cs:ce].indirect(ls), t.pw[:, cs:ce].indirect(ls), (("pgi", cs, ce), ("pw", cs, ce), LS)
            else:
                mi = t.mia[:, k0:k0 + H]
                cwin, pwin, rd = X("cc").indirect(mi), X("pc").indirect(mi), (L("cc"), L("pc"), ("mia", k0, k0 + 8))
            gather("v", X("co"), cwin, [rd[0], rd[2]], L("co"), LB)
            gather("s", X("pg_"), pwin, [rd[1], rd[2]], L("pg_"), LB)
            for (n, f, c0) in (("ax", 5.0, float(1 + OFF + THR)), ("cx", 1.0, float(OFF + THR))):
                if s == 0:
                    add("v", lambda n=n, f=f, c0=c0: v.tensor_scalar(X(n), cwin, f, c0, ALU.mult, ALU.add), [rd[0], rd[2]], [L(n)], cg(LB))
                else:
                    add("s", lambda n=n, f=f, c0=c0: sc.activation(X(n), cwin, AF.Copy, bias=c0, scale=f), [rd[0], rd[2]], [L(n)], cg(LB))
            add("s", lambda: sc.activation(X("fq"), X("ax"), AF.Copy, bias=FQ - (2047.5 + OFF + THR) / 4096, scale=1.0 / 4096), [L("ax")], [L("fq")], cv(LB))
            mm(QB, 64, [(t.idb[:], X("pg_"), LB, False, [C("idb"), L("pg_")]), (t.idb[:], t.r16[:], LB, False, [C("r16")])])
            add("v", lambda: v.tensor_copy(X("po"), t[QB][:, 64:64 + LB]), [ALL(QB)], [L("po")], cv(LB))

        def others():
            if s > 0:
                chosen()
            add("v", lambda: v.tensor_tensor(X("se"), X("kc", 0, LB).indirect(t.cl[:]), U, ALU.is_equal), [L("kc", 0, LB), C("cl"), UR], [L("se")], cg(LB))
            if s == N - 1:
                return places(1)
            mm(RB, 256, [(t.idf[:], U, LB, True, [C("idf"), UR]), (t.nbig[:], X("se"), LB, False, [C("nbig"), L("se")])])
            add("v", lambda: v.tensor_tensor_scan(X("kc", LB), t.sm[:], t[RB][:, 256:256 + LB], 0.0, ALU.mult, ALU.max), [C("sm"), ALL(RB)], [L("kc", LB)], cv(LB))
            places(2)
            send(t.ein[:, k1:k1 + 2 * H], t.eout[:, k0:k0 + 2 * H], LS, ("ein", k1, k1 + 8), "e%d_%d" % (s + 1, b), HOP)
            add("v", lambda: v.tensor_tensor(X("lz", 0, H), X("li", 0, H), X("kc", LB + 15, 2 * LB, 128, 16), ALU.subtract), [L("li"), L("kc", LB)], [L("lz")], cv(H))

        def candidates():
            for (n, WIN) in (("pc", "pw"), ("cc", "cw")):
                add("s", [lambda d=d, n=n, WIN=WIN: sc.activation(X(n, 1 - d, 2 * LB, 128, 2), t[WIN][:, cs:ce].indirect(t.ein[:, k1 + H * d:k1 + H * d + H]), AF.Copy) for d in range(2)],
                    [(WIN, cs, ce), ("ein", k1, k1 + 8)], [L(n)], 2 * cg(LB))

        def piece(u):
            p0, p1, DB = 256 * u, 256 * u + 256, "pb%d" % (2 * NB + u)
            mm(DB, 256, [(limt, t.ex[:, cs + p0:cs + p1], 256, False, LIM)])
            mm(DB, 0, [(t.idb[:], X("f", p0, p1), 256, False, [C("idb"), L("f", p0, p1)])], 128, True, False)
            mm(DB, 0, [(t.nid[:], X("gq", p0, p1), 256, False, [C("nid"), L("gq", p0, p1)])], 128, False, True)
            add("s", lambda: sc.activation(X("a", p0, p1), t[DB][:, 0:256], AF.Abs, scale=1.0 / WT), [ALL(DB)], [L("a", p0, p1)], cv(256))
            add("v", lambda: v.tensor_tensor(X("m", p0, p1), X("a", p0, p1), t[DB][:, 256:512], ALU.is_le), [L("a", p0, p1), ALL(DB)], [L("m", p0, p1)], cv(256))

        def count():
            mm(QB, 224 + 8 * st, [(X("pa"), t.bo[:, 0::16], 8, False, [L("pa"), C("bo")])], LB)

        def key_and_hop():
            mk, rb = X("mk", 0, 128, LB), X("rb", 0, LB, LB)
            count()
            mm(QB, 256, [(X("pa"), t.bo[:], 128, False, [L("pa"), C("bo")])], LB)
            add("v", lambda: v.tensor_reduce(X("pr", 0, 1, LB), t[QB][0:LB, 224:240], AxisListType.X, ALU.mult), [ALL(QB)], [L("pr")], cv(16))
            add("v", lambda: v.tensor_tensor(mk, t.ml[0:LB, :], t[QB][0:LB, 256:384], ALU.mult), [ALL(QB), C("ml")], [L("mk")], cv(128))
            add("v", lambda: v.tensor_scalar(rb, t.e4[0:LB, :], X("pr", 0, 1, LB), 0.0, ALU.mult, ALU.is_lt), [C("e4"), L("pr")], [L("rb")], cv(LB))
            if s < N - 1:
                mm(QB, 384, [(t.idb[:], t.cz[:], H, False, [C("idb"), C("cz")]), (t.oneb[0:1, :], t.cy[0:1, :], H, False, [C("oneb"), C("cy")]),
                             (t.idz[:], X("lz", 0, H), H, True, [C("idz"), L("lz")]), (mk, t.e4z[0:LB, 0::16], H, False, [L("mk"), C("e4z")])], 128, True, False)
                mm(QB, 384, [(t.mlz[0:LB, :], X("rb", 0, LB, LB, 16), H, False, [C("mlz"), L("rb")])], 128, False, True)
                add("v", lambda: v.tensor_scalar(t.mxo[:, k0:k0 + H], t[QB][:, 384:384 + H], MAGIC, MAGIC, ALU.add, ALU.subtract), [ALL(QB)], [("mxo", k0, k0 + 8)], cv(8))
                send(t.mia[:, k1:k1 + H], t.mxo[:, k0:k0 + H], ("mxo", k0, k0 + 8), ("mia", k1, k1 + 8), "k%d_%d" % (s + 1, b), HOP)
            add("v", lambda: v.tensor_scalar(X("f8", 0, 16, LB), t[QB][0:LB, 224:240], 2.0, 0.0, ALU.mult, ALU.max), [ALL(QB)], [L("f8")], cv(16))
            old = [(t.idf[:], t.ck2[:], LB, True, [C("idf"), C("ck2")]), (t.idn[:], U, LB, True, [C("idn"), UR])]
            new = [(mk, t.e4n[0:LB, :], LB, False, [L("mk"), C("e4n")]), (t.mln[0:LB, :], rb, LB, False, [C("mln"), L("rb")])]
            grown = [(t.idf[:], U, LB, True, [C("idf"), UR]), (t.mlp[0:LB, :], t.e4[0:LB, :], LB, False, [C("mlp"), C("e4")])]
            late = [(t.mlp[0:LB, :], rb, LB, False, [C("mlp"), L("rb")]), (t.idf[:], X("w"), LB, True, [C("idf"), L("w")])]

            def change(bank):
                add("v", lambda: v.tensor_tensor(X("w"), X("se"), t[bank][:, 256:256 + LB], ALU.mult), [L("se"), ALL(bank)], [L("w")], cv(LB))

            def matches():
                mm(QB, 128 + LB, [(t.idf[0:LB, :], t.minb[0:LB, o + LB:o + MW], 8, True, [C("idf"), ("minb", o + LB, o + MW)])] +
                   [(t.idb[0:LB, :], X("f8", 8 * k, 8 * k + 8, LB), 8, False, [C("idb"), L("f8")]) for k in range(2)])
            hs = "h%d_%d" % (s + 1, b)
            if s < N - 1:
                mm(QB, 256, old[:1], 128, True, False)
                mm(QB, 256, old[1:] + new, 128, False, True)
                change(QB)
                matches()
                mm(QB, 128, grown + late)
                no = o + MW * NB
                add("s", lambda: sc.activation(t.mout[:, o:o + MW], t[QB][:, 128:128 + MW], AF.Copy), [ALL(QB)], [("mout", o, o + MW)], cv(MW))
                send(t.minb[:, no:no + MW], t.mout[:, o:o + MW], ("mout", o, o + MW), ("minb", no, no + MW), hs, HOP + 0.5)
            else:
                mm(RB, 256, old, 128, True, False)
                matches()
                mm(QB, 128, grown + [(t.idn[:], t.ck[:], LB, True, [C("idn"), C("ck")])], 128, True, False)
                mm(RB, 256, new, 128, False, True)
                change(RB)
                mm(QB, 128, late, 128, False, True)
                f0 = MW * b
                add("s", [lambda: sc.activation(t.fout[:, f0 + LB:f0 + MW], t[QB][:, 128 + LB:128 + MW], AF.Copy)] +
                    [lambda j=j: sc.activation(t.fout[:, f0 + j:f0 + LB:H], t[QB][:, 128 + 16 * j:144 + 16 * j], AF.Copy, scale=1.0 / 1024) for j in range(H)],
                    [ALL(QB)], [("fout", f0, f0 + MW)], (H + 1) * cv(16))
                send(t.fin[:, f0:f0 + MW], t.fout[:, f0:f0 + MW], ("fout", f0, f0 + MW), ("fin", f0, f0 + MW), hs, HOP + 0.5)

        def passed():
            add("v", lambda: v.tensor_scalar(X("pa"), t[RB][:, 0:LB], float(THR + OFF), 31.0 / 32, ALU.is_ge, ALU.subtract), [ALL(RB)], [L("pa")], cv(LB))

        def low():
            add("v", lambda: v.tensor_scalar(X("ci"), X("yi"), 4095, None, ALU.bitwise_and), [L("yi")], [L("ci")], cv(LB))
        if st == 0:
            head()
        for n in ("f", "gq"):
            l0 = 0
            for (k, q) in ((CUTS[b][st], "s"), (32 - CUTS[b][st], "v")) * 2:
                win, WIN, off = (t.xw[:, 0:4096 << st], ("xw", 0, 4096 << st), "co") if n == "f" else (X("f", 0, 16 * (l0 + k)), L("f", 0, 16 * (l0 + k)), "po")
                gather(q, X(n, 16 * l0, 16 * (l0 + k)), win.indirect(X(off, l0, l0 + k)), [WIN, L(off, l0, l0 + k)], L(n, 16 * l0, 16 * (l0 + k)), 16 * k)
                l0 += k
        for u in range(H):
            piece(u)
        if st == 1:
            add("s", lambda: sc.activation(X("ax"), X("cf"), AF.Copy, bias=float(1 + OFF + THR), scale=5.0), [L("cf")], [L("ax")], cv(LB))
        mm(RB, 0, [(t.idf[:], X("ax"), LB, True, [C("idf"), L("ax")]), (t.thb[0:1, :], t.oneb[0:1, 0:LB], LB, False, [C("thb"), C("oneb")])], 128, True, False)
        for n in "am":
            mm(RB, 0, [(t.es[:, 128 * k:128 * k + 128], X(n, k, CB, 128, 16), LB, False, [C("es"), L(n)]) for k in range(16)], 128, False, n == "m")
        if st == 0:
            mm(QB, 128, [(t.idf[:], X("ax"), LB, True, [C("idf"), L("ax")]), (t.n4k[:], X("fq"), LB, False, [C("n4k"), L("fq")])], 128, True, False)
            passed()
            add("v", lambda: v.tensor_tensor(X("yi"), X("cx"), t[RB][:, 0:LB], ALU.min), [L("cx"), ALL(RB)], [L("yi")], cv(LB))
            low()
            mm(QB, 128, [(t.bk[:], X("pa"), LB, False, [C("bk"), L("pa")])], 128, False, True)
            add("v", lambda: v.tensor_tensor(X("cf"), X("ci"), t[QB][:, 128:128 + LB], ALU.max), [L("ci"), ALL(QB)], [L("cf")], cv(LB))
            add("v", lambda: v.tensor_copy(X("co"), X("cf")), [L("cf")], [L("co")], cv(LB))
            count()
            others()
        else:
            passed()
            add("v", lambda: v.tensor_tensor(X("bm"), X("ax"), t[RB][:, 0:LB], ALU.min), [L("ax"), ALL(RB)], [L("bm")], cv(LB))
            key_and_hop()
            mm(RB, 128, [(t.idf[:], X("cf"), LB, True, [C("idf"), L("cf")]), (t.bq[:], X("pa"), LB, False, [C("bq"), L("pa")])])
            add("v", lambda: v.tensor_tensor(X("yi"), X("bm"), t[RB][:, 128:128 + LB], ALU.min), [L("bm"), ALL(RB)], [L("yi")], cv(LB))
            low()
            add("v", lambda: v.tensor_copy(t.cw[:, cs:ce].indirect(ls), X("ci")), [L("ci"), LS], [("cw", cs, ce)], 0.05 + 3.8 * LB * CYC)
            if s < N - 1:
                candidates()
            else:
                add("y", lambda: g.sync.dma_start(t.yg[:, cs:ce], t.cw[:, cs:ce]), [("cw", cs, ce)], (), 0.06, nm("oyg", b), 16, (), 4.0)

    for s in range(N):
        for st in range(2):
            for b in range(NB):
                cur[:] = [NB * s + b, st, {}]
                block_step(s, b, st)
    cur[:] = [NB * N + 2, -1, {}]

    def home(b):
        L, X = tiles(b)
        RB, QB = BANK[b]
        f0 = MW * b
        FR = ("fin", f0, f0 + MW)
        mm(QB, 256, [(t.fin[:, f0:f0 + LB], t.idb[:], 128, False, [FR, C("idb")])], LB)
        mm(RB, 0, [(t.fin[0:LB, f0 + LB:f0 + MW], t.idb[0:LB, 0:LB], LB, False, [FR, C("idb")])], 8)
        add("v", lambda: v.tensor_copy(X("vo", 0, 128, LB), t[QB][0:LB, 256:384]), [ALL(QB)], [L("vo")], cv(128))
        add("s", lambda: sc.activation(X("yo", 0, LB, 8), t[RB][0:8, 0:LB], AF.Copy), [ALL(RB)], [L("yo")], cv(64))
        for (q, k0) in (("y", 0), ("s", 4)):
            add(q, [lambda k=k, q=q: eng[q].dma_start(t.yv[16 * k:16 * k + 16, LB * b:LB * b + LB], X("vo", 16 * k, 16 * k + 16, LB)) for k in range(k0, k0 + 4)],
                [L("vo")], (), 0.24, nm("oyv", b), 64 if q == "y" else 128, (), 2.0)
        add("y", lambda: g.sync.dma_start(t.ym[:, LB * b:LB * b + LB], X("yo", 0, LB, 8)), [L("yo")], (), 0.06, nm("oym", b), 16, (), 2.0)
    for b in range(NB):
        home(b)

    order = schedule(nodes)
    pos = {i: k for k, i in enumerate(order)}
    cnt, known, tok, total = {}, {q: {} for q in eng}, {}, {}
    for i in order:
        d = nodes[i]
        q = d["q"]
        if q == "r":
            tok[i] = (d["sem"], d["val"], {})
            total[d["sem"]] = d["val"]
            continue
        kn = known[q]
        for j in sorted(d["dep"], key=lambda j: -pos[j]):
            if not d["dep"][j]:
                continue
            sem, val, jk = tok[j]
            if kn.get(sem, 0) >= val:
                continue
            eng[q].wait_ge(t.sem[sem], val)
            for (a, w) in list(jk.items()) + [(sem, val)]:
                kn[a] = max(kn.get(a, 0), w)
        for f in d["f"]:
            ins = f()
            if d["sem"] and d["val"] > 0:
                ins.then_inc(t.sem[d["sem"]], 16)
            if d["sem"] is None and (q != "t" or f is d["f"][-1]):
                cnt[csem[q]] = cnt.get(csem[q], 0) + 1
                ins.then_inc(t.sem[csem[q]], 1)
        if d["sem"] is None:
            sem = csem[q]
            tok[i] = (sem, cnt[sem], dict(kn))
            total[sem] = cnt[sem]
        elif d["val"] > 0:
            tok[i] = (d["sem"], d["val"], dict(kn))
            total[d["sem"]] = max(d["val"], total.get(d["sem"], 0))
        else:
            total[d["sem"]] = total.get(d["sem"], 0) - d["val"]
    for sem in total:
        if known["g"].get(sem, 0) < total[sem]:
            g.wait_ge(t.sem[sem], total[sem])
